import numpy as np, ml_dtypes
CORES = [1,5,17,21,33,37,49,53]
N = 8
BF = ml_dtypes.bfloat16
VX, VY, C, B, LE = 2048, 4096, 256, 2, 5
def parts(rng):
    X = rng.integers(0, 256, (N, 8, 16, VX)); Y = rng.integers(0, 256, (N, 8, 16, VY))
    K = rng.integers(0, VX, (N, 8, 16, C)); G = rng.integers(0, VY, (N, 8, 16, B * C)); W = rng.integers(0, VX, (N, 8, 16, B * C))
    z = rng.integers(0, 256, (N, 8, 16, C)); w = rng.integers(0, 64, (N, 8, 16, 1)); t = rng.integers(1000, 1451, (N, 8, 16, 1))
    return X, Y, K, G, W, z, w, t
def pack(X, Y, K, G, W, z, w, t):
    fl = lambda a: np.ascontiguousarray(np.reshape(a, (N, 128, -1))).astype(np.float32).astype(BF)
    wh = lambda a: np.ascontiguousarray(np.reshape(a, (N, 128, -1))).astype(np.int32)
    return {"gx": fl(X), "sy": fl(Y), "rk": wh(K), "rt": wh(G), "wr": wh(W), "z0": fl(z), "wt": fl(w), "th": wh(t)}
def setup_inputs(rng):
    return pack(*parts(rng))
def uneven(rng, top, bits, shape):
    v = np.exp2(bits * rng.random(shape)).astype(np.int64) - 1
    return np.minimum(np.maximum(np.where(rng.random(shape) < 0.5, v, top - v), 0), top)
def setup_inputs_spread(rng):
    X, Y, K, G, W, z, w, t = parts(rng)
    X = (np.exp2(8 * rng.random((N, 8, 1, VX))) * rng.random(X.shape)).astype(np.int64)
    Y = (np.exp2(8 * rng.random((N, 8, 1, VY))) * rng.random(Y.shape)).astype(np.int64)
    z = (np.exp2(8 * rng.random((N, 8, 1, C))) * rng.random(z.shape)).astype(np.int64)
    lx = VX.bit_length() - 1; ly = VY.bit_length() - 1
    K = uneven(rng, VX - 1, lx, K.shape); W = uneven(rng, VX - 1, lx, W.shape); G = uneven(rng, VY - 1, ly, G.shape)
    w = uneven(rng, 63, 6, w.shape); t = rng.integers(0, 4081, t.shape)
    return pack(X, Y, K, G, W, z, w, t)
def setup_inputs_ends(rng):
    sh = np.array([0.0, 0.1, 0.5, 0.9, 1.0])
    X = 255 * (rng.random((N, 8, 16, VX)) < rng.choice(sh, (N, 8, 1, VX))); Y = 255 * (rng.random((N, 8, 16, VY)) < rng.choice(sh, (N, 8, 1, VY)))
    K = (VX - 1) * rng.integers(0, 2, (N, 8, 16, C)); G = (VY - 1) * rng.integers(0, 2, (N, 8, 16, B * C)); W = (VX - 1) * rng.integers(0, 2, (N, 8, 16, B * C))
    z = 255 * rng.integers(0, 2, (N, 8, 16, C)); w = 63 * rng.integers(0, 2, (N, 8, 16, 1)); t = 4080 * (rng.random((N, 8, 16, 1)) < 0.75)
    w[:, :, 0] = 63; w[:, 0, 1] = 0; t[:, 0] = 4080; t[:, 3, :4] = 0
    for q in range(N):
        for g in range(7):
            m = (q + g) % 4
            if m == 0: X[q, g, :, 0] = 0; X[q, g, :, VX - 1] = 255
            if m == 1: X[q, g, :, 0] = 255; X[q, g, :, VX - 1] = 0
            if m == 2: X[q, g, :, 0] = 255 * rng.integers(0, 2, 16); X[q, g, :, VX - 1] = 255
            if m == 3: X[q, g, :, 0] = 255 * rng.integers(0, 2, 16); X[q, g, :, VX - 1] = 255 * rng.integers(0, 2, 16)
    m1 = [m for m in range(1, 17) if (((((255 * 63 * m) & 4095) ** 2) >> 5) & (B - 1)) == B - 1][0]
    s1 = (VY - 1 + 37 * ((255 * 63 * m1) & 4095)) & (VY - 1)
    X[:, 7, :, 0] = 0; X[:, 7, :, VX - 1] = 255; Y[:, 7, :, 0] = 0; Y[:, 7, :, VY - 1] = 255; Y[:, 7, :, s1] = 255; w[:, 7] = 63; t[:, 7] = 4080
    for i, m in ((C - 1, m1), (C - 2, 0), (C - 3, 13), (C - 4, 16), (0, m1), (1, 0), (2, 16)):
        z[:, 7, :, i] = 255 * (np.arange(16) < m)
        K[:, 7, 15, i] = 0; K[:, 7, 14, i] = VX - 1; K[:, 7, 0, i] = 0; G[:, 7, 14:, B * i:B * i + B] = VY - 1; G[:, 7, 0, B * i:B * i + B] = VY - 1
    return pack(X, Y, K, G, W, z, w, t)
def setup_inputs_corners(rng):
    X, Y, K, G, W, z, w, t = parts(rng); h = VX // 2; v = VY // 4
    X[..., :h] = rng.integers(0, 48, (N, 8, 16, h)); X[..., h:] = rng.integers(208, 256, (N, 8, 16, VX - h)); Y[..., :v] = rng.integers(0, 48, (N, 8, 16, v))
    kind = rng.integers(0, 8, (N, 8, 1, C)); kind[..., :8] = np.arange(8); kind[..., C - 8:] = np.arange(8)
    k = np.arange(16)[:, None]; lane = rng.integers(0, 16, (N, 8, 1, C))
    up = ((kind == 1) & (k == 0)) | ((kind == 2) & (k == 15)) | ((kind == 3) & (k == lane)) | ((kind == 4) & (k <= lane))
    lh = np.where(up, rng.integers(h, VX, K.shape), rng.integers(0, h, K.shape))
    K = np.where(kind == 7, (VX - 1) * rng.integers(0, 2, K.shape), np.where(kind == 6, K, lh))
    z = np.where(kind < 5, rng.integers(64, 96, z.shape), np.where(kind == 5, 255, np.where(kind == 6, 0, z)))
    M = np.zeros((8, 16), np.int64); M[1] = 4080; M[7] = 4080; M[2, 15] = 4080; M[3, 0] = 4080; M[4, ::2] = 4080; M[5, :15] = 4080
    mode = (np.arange(N)[:, None] + np.arange(8)) % 8
    t = np.where((mode == 6)[:, :, None, None], rng.choice(np.array([0, 1, 4079, 4080, 1300]), t.shape), M[mode][..., None])
    q = rng.permutation(N); t[q[0]] = 0; t[q[1]] = 4080
    a = rng.integers(0, 3, (N, 8, 1, 1)); a[:, 0] = 0; a[:, 7] = 1; w = np.where(a == 0, 0, np.where(a == 1, 63, w))
    W = np.where(rng.random((N, 8, 1, 1)) < 0.4, (VX - 1) * rng.integers(0, 2, W.shape), W)
    G = np.where(rng.random((N, 8, 1, 1)) < 0.4, (VY - 1) * rng.integers(0, 2, G.shape), G)
    z[q[1], ::2] = 0
    e = int(q[2])
    X[e] = np.minimum(X[e], 254); Y[e] = rng.integers(0, 61, Y[e].shape); K[e] = rng.integers(0, h, K[e].shape); z[e] = 255; t[e] = rng.integers(2900, 3301, t[e].shape)
    b = int(q[3]); gb = (7 - b) % 8
    X[b, gb] = np.minimum(X[b, gb], 254); z[b, gb] = 255
    return pack(X, Y, K, G, W, z, w, t)
def setup_inputs_ties(rng):
    X, Y, K, G, W, z, w, t = parts(rng)
    X[:, ::2] = 128 * rng.integers(0, 2, (N, 4, 16, VX)); Y[:, ::2] = 128 * rng.integers(0, 2, (N, 4, 16, VY))
    X[:, 1::2] = 85 * rng.integers(0, 4, (N, 4, 16, VX)); Y[:, 1::2] = 85 * rng.integers(0, 4, (N, 4, 16, VY))
    z[:, ::2] = 16 * rng.integers(0, 9, (N, 4, 16, C)); z[:, 1::2] = np.maximum(85 * rng.integers(0, 4, (N, 4, 16, C)) - 16 * rng.integers(0, 8, (N, 4, 16, C)), 0)
    t[:, ::2] = 128 * rng.integers(6, 12, (N, 4, 16, 1)); t[:, 1::2] = 85 * rng.integers(17, 24, (N, 4, 16, 1))
    t = t + rng.integers(-1, 2, t.shape) * (rng.random(t.shape) < 0.5)
    X[:, 5] = rng.integers(200, 256, (N, 16, VX)); Y[:, 5] = rng.integers(0, 61, (N, 16, VY))
    X[:, 6] = rng.integers(0, 61, (N, 16, VX)); Y[:, 6] = rng.integers(200, 256, (N, 16, VY))
    t[:, 5:7] = 3160 + rng.integers(-300, 151, (N, 2, 16, 1))
    return pack(X, Y, K, G, W, z, w, t)
def setup_inputs_alike(rng):
    X, Y, K, G, W, z, w, t = parts(rng)
    K[:, ::2] = K[:, ::2, :1, :].copy(); K[:, 1] = K[:, 1, :, :1].copy(); W[:, 1] = W[:, 1, :, :1].copy()
    W[:, 2:4] = np.repeat(K[:, 2:4], B, axis=-1); G[:, 4] = G[:, 4, :1, :1].copy(); z[:, 5] = z[:, 5, :, :1].copy()
    few = np.array([0, VX - 1, VX // 2, 3]); K[:, 7] = rng.choice(few, (N, 16, C)); W[:, 7] = rng.choice(few, (N, 16, B * C))
    return pack(X, Y, K, G, W, z, w, t)
def check_inputs(d):
    bad = []
    for k, hi in (("gx", 255), ("sy", 255), ("rk", VX - 1), ("rt", VY - 1), ("wr", VX - 1), ("z0", 255), ("wt", 63), ("th", 4080)):
        a = np.asarray(d[k]).astype(np.float64)
        if not (np.min(a) >= 0 and np.max(a) <= hi): bad.append("range of " + k)
        elif not np.all(a == np.floor(a)): bad.append("whole numbers of " + k)
    return bad
def reference(gx, sy, rk, rt, wr, z0, wt, th):
    ints = lambda a, n: a.astype(np.float32).astype(np.int32).reshape(N, 8, 16, n)
    X, Y, z, w = ints(gx, VX), ints(sy, VY), ints(z0, C), ints(wt, 1)
    K = rk.astype(np.int64).reshape(N, 8, 16, C); G = rt.astype(np.int64).reshape(N, 8, 16, B * C); W = wr.astype(np.int64).reshape(N, 8, 16, B * C)
    t = th.astype(np.int64).reshape(N, 8, 16, 1); A = np.zeros((N, 1, 1, 1), np.int64)
    margin = (16 * ((15 - np.arange(16)) >> 1)).astype(np.int32)[:, None]
    for lead in range(LE):
        if lead > 0: K = np.roll(K, 1, axis=0); z = np.roll(z, 1, axis=0)
        u = np.add.reduce(w.astype(np.int64) * z, axis=2) & 4095
        c = B * np.arange(C) + (((u * u) >> 5) & (B - 1)); cc = np.broadcast_to(c[:, :, None, :], K.shape)
        route = np.take_along_axis(G, cc, 3); old = np.take_along_axis(W, cc, 3)
        s = (((route * K) >> 5) + route + 37 * u[:, :, None, :]) & (VY - 1)
        x = np.take_along_axis(X, K.reshape(N, 8, 1, 16 * C), 3).reshape(N, 8, 16, 16, C)
        y = np.take_along_axis(Y, s.reshape(N, 8, 1, 16 * C), 3).reshape(N, 8, 16, 16, C)
        placed = np.add.reduce(np.abs(x - y), axis=2) < t + A
        hold = placed & (np.count_nonzero(x >= z[:, :, :, None, :] + margin, axis=2) >= 9)
        stop = np.logical_or.accumulate(hold[:, :, ::-1], axis=2)[:, :, ::-1]
        held = placed & stop; fail = placed & ~stop
        h, f, o = held.astype(np.int64), fail.astype(np.int64), 1 - placed.astype(np.int64)
        nh = np.add.reduce(h, axis=2)[:, :, None]; nf = np.add.reduce(f, axis=2)[:, :, None]
        over = np.add.accumulate(h[:, :, ::-1], axis=2)[:, :, ::-1] - h
        pos = np.where(held, over, np.where(fail, nh + np.add.accumulate(f, axis=2) - f, nh + nf + np.add.accumulate(o, axis=2) - o))
        new = np.zeros_like(K); np.put_along_axis(new, pos, np.where(fail, old, K), 2)
        np.put_along_axis(W, cc, np.where(fail, K, old), 3)
        z = np.abs(z - np.maximum.reduce(np.where(held[:, :, None], x, 0), axis=3))
        A = 16 * (np.add.reduce(f, axis=(1, 2, 3)) & 31).reshape(N, 1, 1, 1)
        K = new
    return {"yk": K.reshape(N, 128, C).astype(np.float32), "yw": W.reshape(N, 128, B * C).astype(np.float32), "yz": z.reshape(N, 128, C).astype(np.float32).astype(BF)}

@@ -1,0 +1,531 @@
+from concourse.bass import DstId, RemoteDMATransfer
+from concourse.mybir import dt, AluOpType as OP, AxisListType, ActivationFunctionType as AF
+
+VX, VY, C, LE = 2048, 4096, 256, 5
+NCH = 2
+n = C // NCH
+SB = 64
+NS_ = n // SB
+nq = n // 16
+PAD = 32
+KB = 512 // n
+NB = 16 // KB
+ABS_S = (0,)
+CFG = {"fix": {"V": 0.03, "S": 0.05, "P": 0.0, "G": 0.05, "D": 0.06, "E": 0.06}, "pe": 0.417e-3, "cy": 0.83e-3 * 1.25, "ga": 1.56,
+       "sc": 3.8, "wake": 0.08, "net": 2.6, "jit": 0.0}
+
+
+UF = 256
+FB = 4 * ((NCH - 1) % 2)
+CUR = {"lc": (0, 0)}
+CACHE = {}
+BIAS = {("UL", 0): -17.0, ("x", 0): 5.0, ("xz", 0): -1.9, ("sg", 0): 15.0, ("cnt", 0): -12.2, ("y", 0): 40.4, ("abs", 0): -0.9, ("D", 0): 14.1, ("relu", 0): 39.5,
+        ("mk", 0): 6.4, ("wg", 0): 8.4, ("dk", 0): -4.9, ("va", 0): -20.3, ("E", 0): 7.3, ("xh", 0): -24.3, ("scan", 0): -0.8, ("clamp", 0): 0.6, ("NM", 0): -24.8,
+        ("scat", 0): 17.4, ("K'", 0): -3.6, ("UL", 1): 1.8, ("D", 1): -5.6, ("scan", 1): -10.1, ("R", 1): 3.3, ("relu", 1): -7.6, ("scat", 1): 1.1, ("E", 1): -7.5,
+        ("va", 1): -1.1, ("z'", 1): 10.5, ("fd", 1): -11.2, ("P", 1): 16.2, ("cd", 1): 3.7, ("K'", 1): 8.0, ("NM", 1): 0.5, ("abs", 1): -6.7, ("cnt", 1): -2.0,
+        ("dk", 1): -7.1, ("sg", 1): 6.2, ("wg", 1): -1.7, ("x", 1): -6.6, ("xz", 1): 6.9}
+
+
+def two(name, dtype, cols):
+    return {name: ("sbuf", [128, cols], dtype)}
+
+
+SCRATCH = {}
+for _nm, _dt, _co in (
+        ("gearb", "bfloat16", PAD + VX), ("siteb", "bfloat16", VY), ("rkb", "int32", C), ("rtb", "int32", 2 * C), ("wri", "int32", 2 * C),
+        ("wrb", "float32", 2 * C), ("wtb", "bfloat16", 2), ("thb", "int32", 2), ("tcol", "float32", 2), ("tac", "float32", 8),
+        ("lst", "uint16", LE * C), ("lsend", "uint16", LE * C), ("zb", "bfloat16", LE * C), ("zsend", "bfloat16", LE * C),
+        ("ci", "int32", 2 * NCH * nq), ("v5", "int32", 2 * NCH * nq), ("vv", "int32", 2 * NCH * nq), ("bi", "int32", 2 * NCH * nq),
+        ("cc", "int32", 2 * NCH * nq), ("cl", "uint16", 2 * C),
+        ("k32", "float32", 2 * C), ("k16", "float16", 2 * C), ("pp", "int32", 2 * C), ("qq", "int32", 2 * C), ("tt", "int32", 2 * C),
+        ("t2", "int32", 2 * C), ("sl", "uint16", 2 * C),
+        ("xx", "bfloat16", 32 * C), ("dd", "bfloat16", 32 * C), ("da", "bfloat16", 32 * C), ("sg", "bfloat16", 32 * C),
+        ("pm", "bfloat16", 2 * C), ("hd", "bfloat16", 2 * C), ("ff", "bfloat16", 2 * C), ("mk", "float32", 2 * C), ("hl", "uint16", 2 * C),
+        ("xh", "bfloat16", 32 * C), ("xs", "bfloat16", 32 * C), ("rr", "bfloat16", 4 * C), ("po", "bfloat16", 2 * C),
+        ("wg", "float32", 2 * C), ("dk", "float32", 2 * C), ("fd", "float32", 2 * C), ("va", "float16", 2 * C), ("kl", "float16", 32 * C),
+        ("yks", "float32", C), ("yws", "float32", 2 * C),
+        ("fs", "bfloat16", LE * NCH), ("fi", "int32", LE), ("fm", "int32", LE),
+        ("one", "bfloat16", 2048), ("b1", "bfloat16", 144), ("b2", "bfloat16", 144), ("bn", "bfloat16", 144), ("bh", "bfloat16", 144),
+        ("bw", "bfloat16", 144), ("tmpa", "bfloat16", 144), ("tmpb", "bfloat16", 144), ("tmpc", "bfloat16", 128),
+        ("blk", "bfloat16", 128), ("idn", "bfloat16", 128), ("idm", "bfloat16", 128), ("i16", "bfloat16", 128), ("i20", "bfloat16", 128),
+        ("i64", "bfloat16", 128), ("im64", "bfloat16", 128), ("i384", "bfloat16", 128),
+        ("tri", "bfloat16", 128), ("tri4", "bfloat16", 128), ("low", "bfloat16", 128), ("upp", "bfloat16", 128), ("upm", "bfloat16", 128),
+        ("bk", "bfloat16", 2048), ("bp", "bfloat16", 2048), ("mb0", "bfloat16", 128), ("mb1", "bfloat16", 128),
+        ("w37", "float32", 2), ("wa", "bfloat16", 2), ("wb", "float32", 2), ("wac", "float32", 2), ("wcol", "float32", 2),
+        ("lwa", "bfloat16", 128), ("lwb", "bfloat16", 128),
+        ("rst", "bfloat16", 16 * n), ("io2", "int32", nq), ("kf", "float32", 2), ("cz", "float32", 8),
+        ("c64", "float32", 2), ("c15", "float32", 2), ("cnm", "float32", 2), ("cny", "float32", 2)):
+    SCRATCH.update(two(_nm, _dt, _co))
+for _b in range(8):
+    SCRATCH["ps%d" % _b] = ("psum", [128, 512], "float32")
+
+LOADS = ("gear", "site", "rk", "rt", "wr", "z", "wt", "th")
+SEMAPHORES = ["sV", "sS", "sP", "sG", "sent"] + ["ld_" + x for x in LOADS] + ["st%d" % i for i in range(3 * NCH)]
+SEMAPHORES += ["a%s%d_%d" % (k, e, c) for k in "kz" for e in range(1, LE) for c in range(NCH)]
+
+
+def sl(T, name, a, b, st=1):
+    return T[name][:, a:b] if st == 1 else T[name][:, a:b:st]
+
+
+def build():
+    ops = []
+    cy, ga, fix = CFG["cy"], CFG["ga"], CFG["fix"]
+
+    def add(eng, cost, fn, rd=(), wr=(), bank=(), name="", lat=0.0, sem=None, inc=1, acc=None):
+        ops.append({"e": eng, "dur": cost + fix[eng], "fn": fn, "rd": list(rd), "wr": list(wr), "bank": list(bank), "name": name,
+                    "lat": lat, "sem": sem, "inc": inc, "lc": CUR["lc"], "acc": acc})
+
+    def vcost(m, cyc=1.0):
+        return max(64, m * cyc) * cy
+
+    def gcost(m):
+        return 0.04 + m * ga * cy
+
+    def pcost(*cols):
+        return sum(max(64, x) for x in cols) * CFG["pe"] * 1.25
+
+    def load(q, dst, src, a, b, key, lat):
+        add(q, 0.0, lambda g, T, e: e.dma_start(sl(T, dst, a, b), T[src][:]), wr=[dst] if dst != "zb" else [("zb", 0, c) for c in range(NCH)],
+            name="load " + src, lat=lat, sem="ld_" + key, inc=16)
+    load("D", "wtb", "wt", 0, 1, "wt", 2.0)
+    load("E", "zb", "z0", 0, C, "z", 2.0)
+    load("D", "rkb", "rk", 0, C, "rk", 2.2)
+    load("D", "gearb", "gx", PAD, PAD + VX, "gear", 4.5)
+    load("E", "rtb", "rt", 0, 2 * C, "rt", 3.5)
+    load("E", "thb", "th", 0, 1, "th", 4.0)
+    load("D", "siteb", "sy", 0, VY, "site", 8.0)
+    load("E", "wri", "wr", 0, 2 * C, "wr", 4.0)
+
+    def aff(dst, src, m, pat, cmp_, base, cm, w=None):
+        add("G", 0.17 + 2 * m * cy, lambda g, T, e: e.affine_select(sl(T, dst, 0, m), sl(T, src, 0, m), pat, cmp_, 0.0, base, cm),
+            rd=[src], wr=[dst], name="aff " + dst)
+
+    def iot(dst, m, pat, base, cm):
+        def f(g, T, e):
+            if SCRATCH[dst][2] == "int32":
+                return e.iota(sl(T, dst, 0, m), pat, base, cm)
+            return e.iota(sl(T, dst, 0, m), pat, base, cm, allow_small_or_imprecise_dtypes=True)
+        add("G", 0.13 + 2 * m * cy, f, wr=[dst], name="iota " + dst)
+
+    def ts(dst, a, b, src, c0, d, s1, s2, o1, o2=None, rd=None, wr=None, cyc=1.0, bank=(), eng="V", st=1, sst=1, dst_st=1):
+        def f(g, T, e):
+            x1 = s1(T) if callable_(s1) else s1
+            x2 = s2(T) if callable_(s2) else s2
+            if o2 is None:
+                return e.tensor_scalar(sl(T, dst, a, b, dst_st), sl(T, src, c0, d, sst), x1, None, o1)
+            return e.tensor_scalar(sl(T, dst, a, b, dst_st), sl(T, src, c0, d, sst), x1, x2, o1, o2)
+        add("V", vcost((b - a) // dst_st, cyc), f, rd=rd, wr=wr, bank=bank, name="ts " + dst)
+
+    def callable_(x):
+        return not isinstance(x, (int, float)) and x is not None
+
+    def cst(dst, src, m, mul, addv=None):
+        if addv is None:
+            ts(dst, 0, m, src, 0, m, mul, None, OP.mult, rd=[src], wr=[dst], cyc=0.5)
+        else:
+            ts(dst, 0, m, src, 0, m, mul, addv, OP.mult, OP.add, rd=[src], wr=[dst])
+
+    add("V", 0.3, lambda g, T, e: e.memset(T.one[:, 0:144], 1.0), wr=["one"], name="one")
+    add("V", vcost(32), lambda g, T, e: e.memset(T.gearb[:, 0:PAD], 0.0), wr=["gpad"], name="gpad")
+    aff("tmpa", "one", 144, [[-16, 9], [0, 16]], OP.is_ge, 0, 1)
+    aff("tmpb", "tmpa", 144, [[16, 9], [0, 16]], OP.is_ge, 15, -1)
+    aff("b1", "tmpb", 144, [[0, 9], [1, 16]], OP.is_equal, -15, 0)
+    ts("wcol", 0, 1, "wtb", 0, 1, 1.0, None, OP.mult, rd=["wtb"], wr=["wcol"])
+    add("V", vcost(144, .5), lambda g, T, e: e.tensor_scalar(T.bw[:, 0:144], T.b1[:, 0:144], T.wcol[:, 0:1], None, OP.mult), rd=["b1", "wcol"], wr=["bw"], name="bw")
+    iot("io2", nq, [[32, nq]], 0, 0)
+    iot("kf", 1, [[0, 1]], 0, 1)
+    ts("w37", 0, 1, "wtb", 0, 1, 37.0, None, OP.mult, rd=["wtb"], wr=["w37"])
+    ts("wa", 0, 1, "w37", 0, 1, 1.0, None, OP.mult, rd=["w37"], wr=["wa"])
+    ts("wac", 0, 1, "wa", 0, 1, 1.0, None, OP.mult, rd=["wa"], wr=["wac"])
+    add("V", vcost(1), lambda g, T, e: e.tensor_tensor(T.wb[:, 0:1], T.w37[:, 0:1], T.wac[:, 0:1], OP.subtract), rd=["w37", "wac"], wr=["wb"], name="wb")
+    add("V", vcost(128, .5), lambda g, T, e: e.tensor_scalar(T.lwa[:, 0:128], T.tmpb[:, 0:128], T.wac[:, 0:1], None, OP.mult), rd=["tmpb", "wac"], wr=["lwa"], name="lwa")
+    add("V", vcost(128, .5), lambda g, T, e: e.tensor_scalar(T.lwb[:, 0:128], T.tmpb[:, 0:128], T.wb[:, 0:1], None, OP.mult), rd=["tmpb", "wb"], wr=["lwb"], name="lwb")
+    add("V", vcost(1), lambda g, T, e: e.tensor_copy(T.ci[:, 0:1], T.kf[:, 0:1]), rd=["kf"], wr=[("ci", 0, 0)], name="k0")
+    ts("v5", 0, 1, "ci", 0, 1, 15, None, OP.bitwise_and, rd=[("ci", 0, 0)], wr=[("v5", 0, 0)])
+    ts("cz", 0, 1, "v5", 0, 1, 1.0, None, OP.mult, rd=[("v5", 0, 0)], wr=["cz"])
+    cst("c64", "cz", 1, 1.0, -64.0)
+    cst("c15", "cz", 1, -1.0, 15.0)
+    cst("cny", "cz", 1, 2048.0, -2048.0 * 15)
+    cst("cnm", "cz", 1, 2048.0, -2048.0 * 15 + PAD)
+    add("V", vcost(nq), lambda g, T, e: e.tensor_scalar(T.cc[:, 0:nq], T.io2[:, 0:nq], T.cz[:, 0:1], T.cz[:, 0:1], OP.add, OP.add), rd=["io2", "cz"],
+        wr=[("cc", 0, 0)], name="io2b")
+    add("V", vcost(nq), lambda g, T, e: e.tensor_copy(T.io2[:, 0:nq], T.cc[:, 0:nq]), rd=[("cc", 0, 0)], wr=["io2"], name="io2c")
+    ts("tcol", 0, 1, "thb", 0, 1, 1.0, None, OP.mult, rd=["thb"], wr=["tcol"])
+    ts("tac", 0, 1, "thb", 0, 1, 1.0, None, OP.mult, rd=["thb"], wr=[("tac", 0)])
+    aff("idn", "one", 128, [[-1, 128]], OP.is_equal, 0, 1)
+    cst("idm", "idn", 128, -1.0)
+    cst("i16", "idn", 128, 16.0)
+    cst("bh", "b1", 144, 0.5)
+    cst("b2", "b1", 144, 2.0)
+    cst("bn", "b1", 144, -1.0)
+    aff("tri", "tmpb", 128, [[-1, 128]], OP.is_ge, 0, 1)
+    cst("tri4", "tri", 128, 4096.0)
+    cst("i20", "idn", 128, 1048576.0)
+    aff("low", "tmpb", 128, [[1, 128]], OP.is_ge, -1, -1)
+    aff("upp", "tmpb", 128, [[-1, 128]], OP.is_ge, -1, 1)
+    cst("upm", "upp", 128, -1.0)
+    cst("i64", "idn", 128, 64.0)
+    cst("im64", "idn", 128, -64.0)
+    cst("i384", "idn", 128, 3840.0)
+    iot("mb0", 128, [[0, 8], [-32, 16]], 0, 0)
+    add("V", vcost(128, 2), lambda g, T, e: e.tensor_tensor(T.mb1[:, 0:128], T.mb0[:, 0:128], T.tmpb[:, 0:128], OP.mult), rd=["mb0", "tmpb"], wr=["mb1"], name="mb1")
+    add("V", vcost(2048, .5), lambda g, T, e: e.memset(T.kl[:, 0:16], 0) if False else e.memset(T.rst[:, 0:16 * n], 1.0), wr=["rst1"], name="rst1")
+    aff_src = "rst1"
+    add("G", 0.17 + 2 * 2048 * cy, lambda g, T, e: e.affine_select(T.bk[:, 0:2048], T.rst[:, 0:2048], [[-1, 16], [-16, 8], [0, 16]], OP.is_equal, 0.0, 0, 1),
+        rd=[aff_src, "upp", "low", "tri", "idn"], wr=["bk"], name="bk")
+    add("V", vcost(n), lambda g, T, e: e.memset(T.rst[:, 0:16 * n:16], 0.0), rd=["rst1", "bk"], wr=["rst", "rst1"], name="rst")
+    for j in range(4):
+        b = j + 2 if j < 2 else j + 4
+
+        def fbp(g, T, e, j=j, b=b):
+            ps = T["ps%d" % b]
+            for k in range(4):
+                e.matmul(ps[:, 128 * k:128 * k + 128], T.i384[:, 0:128], T.bk[:, 512 * j + 128 * k:512 * j + 128 * k + 128], True, False)
+                r = e.matmul(ps[:, 128 * k:128 * k + 128], T.idn[:, 0:128], T.mb1[:, 0:128], False, True)
+            return r
+        add("P", pcost(*[128] * 8), fbp, rd=["i384", "bk", "idn", "mb1"], wr=[("bpp", j)], bank=[b], name="bpp")
+        add("S", 512 * cy, lambda g, T, e, j=j, b=b: e.activation(T.bp[:, 512 * j:512 * j + 512], T["ps%d" % b][:, 0:512], AF.Copy), rd=[("bpp", j)], wr=["bp%d" % j],
+            bank=[b], name="bp")
+    BP = ["bp%d" % j for j in range(4)]
+    for c in range(NCH):
+        i0 = c * n
+        ts("lst", i0, i0 + n, "rkb", i0, i0 + n, float(PAD), None, OP.add, rd=["rkb"], wr=[("lst", 0, c)])
+
+    def wrprep(c):
+        ts("wrb", 2 * c * n, 2 * c * n + 2 * n, "wri", 2 * c * n, 2 * c * n + 2 * n, float(PAD), None, OP.add, rd=["wri"], wr=[("wrb", c)])
+
+    for e_ in range(LE):
+        for c in range(NCH):
+            CUR["lc"] = (e_, c)
+            chunk(add, ts, vcost, gcost, pcost, e_, c, BP, wrprep, cy)
+    return ops
+
+
+def count(add, vcost, pcost, e_):
+    def ff2(g, T, e):
+        ps = T["ps%d" % FB]
+        for c in range(NCH):
+            r = e.matmul(ps[:, UF + 1:UF + 2], T.one[:, 0:128], T.fs[:, e_ * NCH + c:e_ * NCH + c + 1], c == 0, c == NCH - 1)
+        return r
+    add("P", pcost(*[64] * NCH), ff2, rd=["one"] + [("fs", e_, c) for c in range(NCH)], wr=[("f2", e_)], bank=[FB], name="F2")
+    add("V", vcost(1), lambda g, T, e: e.tensor_copy(T.fi[:, e_:e_ + 1], T["ps%d" % FB][:, UF + 1:UF + 2]), rd=[("f2", e_)], wr=[("fi", e_)], bank=[FB], name="fi")
+    add("V", vcost(1), lambda g, T, e: e.tensor_scalar(T.fm[:, e_:e_ + 1], T.fi[:, e_:e_ + 1], 31, None, OP.bitwise_and), rd=[("fi", e_)], wr=[("fm", e_)], name="fm")
+    add("V", vcost(1), lambda g, T, e: e.tensor_scalar(T.tac[:, e_ + 1:e_ + 2], T.fm[:, e_:e_ + 1], 16.0, T.tcol[:, 0:1], OP.mult, OP.add),
+        rd=[("fm", e_), "tcol"], wr=[("tac", e_ + 1)], name="ta")
+
+
+def chunk(add, ts, vcost, gcost, pcost, e_, c, BP, wrprep, cy):
+    i0 = c * n
+    pr = e_ % 2
+    o = pr * C + i0
+    of = 16 * o
+    R0, R1, X0, X1 = 4 * (c % 2), 4 * (c % 2) + 1, 4 * (c % 2) + 2, 4 * (c % 2) + 3
+    lz = e_ * C + i0
+    ot = (pr * NCH + c) * nq
+    last = e_ == LE - 1
+    t = lambda nm, *x: (nm, pr, c) + x
+    L, Z = ("lst", e_, c), ("zb", e_, c)
+
+    def mm(out, lhs, rhs, start, stop):
+        return lambda T, e: e.matmul(out(T), lhs(T), rhs(T), start, stop)
+
+    def PS(b, a, w):
+        return lambda T: T["ps%d" % b][:, a:a + w]
+
+    def M(nm, a=0, w=128):
+        return lambda T: T[nm][:, a:a + w]
+
+    def Sx(nm, a, b, st):
+        return lambda T: T[nm][:, a:b:st]
+
+    def pe(mms, cols, **kw):
+        def f(g, T, e):
+            for m in mms:
+                r = m(T, e)
+            return r
+        add("P", pcost(*cols), f, **kw)
+
+    def group(out, pairs):
+        return [mm(out, l, r, i == 0, i == len(pairs) - 1) for i, (l, r) in enumerate(pairs)]
+
+    def act(out, src, func, m, bias=None, **kw):
+        def f(g, T, e):
+            if bias is None:
+                return e.activation(out(T), src(T), func)
+            return e.activation(out(T), src(T), func, bias=bias(T) if not isinstance(bias, float) else bias)
+        add("S", m * cy, f, **kw)
+
+    def vec(f, m, cyc=1.0, cost=None, **kw):
+        add("V", vcost(m, cyc) if cost is None else cost, lambda g, T, e: f(T, e), **kw)
+
+    pe(group(PS(R0, 0, nq), [(M("bw", 15 - m), Sx("zb", lz + m, lz + n, 16)) for m in range(16)]), [64] * 16, rd=["bw", Z], wr=[t("ul")], bank=[R0], name="UL")
+    vec(lambda T, e: e.tensor_copy(T.ci[:, ot:ot + nq], T["ps%d" % R0][:, 0:nq]), nq, rd=[t("ul")], wr=[t("ci")], bank=[R0], name="ci")
+    vec(lambda T, e: e.tensor_scalar(T.v5[:, ot:ot + nq], T.ci[:, ot:ot + nq], 31, None, OP.bitwise_and), nq, rd=[t("ci")], wr=[t("v5")], name="v5")
+    vec(lambda T, e: e.tensor_tensor(T.vv[:, ot:ot + nq], T.v5[:, ot:ot + nq], T.v5[:, ot:ot + nq], OP.mult), nq, 2, rd=[t("v5")], wr=[t("vv")], name="vv")
+    vec(lambda T, e: e.tensor_scalar(T.bi[:, ot:ot + nq], T.vv[:, ot:ot + nq], 5, 1, OP.arith_shift_right, OP.bitwise_and), nq, rd=[t("vv")], wr=[t("bi")], name="bi")
+    vec(lambda T, e: e.tensor_tensor(T.cc[:, ot:ot + nq], T.bi[:, ot:ot + nq], T.io2[:, 0:nq], OP.add), nq, 2, rd=[t("bi"), "io2"], wr=[t("cc")], name="cc")
+    oc = (pr * NCH + c) * n
+    vec(lambda T, e: e.tensor_copy(T.cl[:, oc:oc + nq], T.cc[:, ot:ot + nq]), nq, rd=[t("cc")], wr=[t("cl")], name="cl")
+    pe(group(PS(R0, 128, n), [(M("lwa"), M("zb", lz, n)), (M("lwb"), M("zb", lz, n))]), [n] * 2, rd=["lwa", "lwb", Z], wr=[t("u37")], bank=[R0], name="U37")
+
+    vec(lambda T, e: e.tensor_copy(T.k32[:, o:o + n], T.lst[:, lz:lz + n]), n, rd=[L], wr=[t("k32")], name="k32")
+    for s in range(NS_):
+        a = of + s * SB * 16
+        add("S", gcost(SB * 16), lambda g, T, e, a=a, s=s: e.activation(T.xx[:, a:a + SB * 16], T.gearb[:, 0:PAD + VX].indirect(T.lst[:, lz + s * SB:lz + s * SB + SB]), AF.Copy),
+            rd=["gearb", "gpad", L], wr=[t("xx", s)], name="x")
+    vec(lambda T, e: e.tensor_tensor(T.pp[:, o:o + n], T.rtb[:, 2 * i0:2 * i0 + 2 * n].indirect(T.cl[:, oc:oc + nq]), T.k32[:, o:o + n], OP.mult), n, cost=gcost(n),
+        rd=["rtb", t("cl"), t("k32")], wr=[t("pp")], name="P")
+    vec(lambda T, e: e.tensor_scalar(T.qq[:, o:o + n], T.pp[:, o:o + n], 5, None, OP.arith_shift_right), n, rd=[t("pp")], wr=[t("qq")], name="Q")
+    vec(lambda T, e: e.tensor_tensor(T.tt[:, o:o + n], T.qq[:, o:o + n], T["ps%d" % R0][:, 128:128 + n], OP.add), n, rd=[t("qq"), t("u37")], wr=[t("tt")], bank=[R0], name="T")
+    vec(lambda T, e: e.tensor_scalar(T.t2[:, o:o + n], T.tt[:, o:o + n], 4095, None, OP.bitwise_and), n, rd=[t("tt")], wr=[t("t2")], name="T2")
+    vec(lambda T, e: e.tensor_copy(T.sl[:, o:o + n], T.t2[:, o:o + n]), n, rd=[t("t2")], wr=[t("sl")], name="SL")
+
+    for j in range(NB):
+        b = (X0, X1)[j % 2]
+        ms, cols = [], []
+        for kk in range(KB):
+            k = j * KB + kk
+            ms += group(PS(b, kk * n, n), [(M("idn"), Sx("xx", of + k, of + 16 * n, 16)), (M("idm"), M("zb", lz, n))])
+            cols += [n, n]
+        pe(ms, cols, rd=["idn", "idm", Z] + [t("xx", s) for s in range(NS_)], wr=[t("xz", j)], bank=[b], name="xz")
+        for h in range(KB // 2):
+            k = j * KB + 2 * h
+            bias = 0.5 - 16 * ((15 - k) // 2)
+            add("S", 2 * n * cy, lambda g, T, e, b=b, h=h, k=k, v=k // 2: e.activation(T.sg[:, of + k * n:of + k * n + 2 * n], T["ps%d" % b][:, 2 * h * n:2 * h * n + 2 * n],
+                AF.Sign, bias=T.mcol[:, v:v + 1] if False else 0.5 - 16 * ((15 - k) // 2)), rd=[t("xz", j)], wr=[t("sg", k // 2)], bank=[b], name="sg")
+        pe([mm(PS(R1, 0, n), M("bh", 15 - k), M("sg", of + k * n, n), k == 0, False) for k in range(j * KB, j * KB + KB)], [n] * KB,
+           rd=["bh"] + [t("sg", v) for v in range(j * KB // 2, j * KB // 2 + KB // 2)], wr=[t("cn", j)], bank=[R1], acc=("cn", e_, c), name="cnt")
+
+    for s in range(NS_):
+        a = of + s * SB * 16
+        w = SB * 16
+        vec(lambda T, e, a=a, w=w, s=s: e.tensor_tensor(T.dd[:, a:a + w], T.siteb[:, 0:VY].indirect(T.sl[:, o + s * SB:o + s * SB + SB]), T.xx[:, a:a + w], OP.subtract), w, cost=gcost(w),
+            rd=["siteb", t("sl"), t("xx", s)], wr=[t("dd", s)], name="y")
+        ab = s in ABS_S
+        if ab:
+            act(M("da", a, w), M("dd", a, w), AF.Abs, w, rd=[t("dd", s)], wr=[t("da", s)], name="abs")
+            pairs = [(M("b1", 15 - k), Sx("da", a + k, a + w, 16)) for k in range(16)]
+        else:
+            vec(lambda T, e, a=a, w=w: e.tensor_scalar(T.da[:, a:a + w], T.dd[:, a:a + w], 0.0, None, OP.max), w, 0.5, rd=[t("dd", s)], wr=[t("da", s)], name="relu")
+            pairs = [(M("bn", 15 - k), Sx("dd", a + k, a + w, 16)) for k in range(16)] + [(M("b2", 15 - k), Sx("da", a + k, a + w, 16)) for k in range(16)]
+        if ab:
+            pe(group(PS(R0, 256 + s * SB, SB), pairs), [SB] * len(pairs), rd=["b1", t("da", s)], wr=[t("D", s)], bank=[R0], name="D")
+        else:
+            pe(group(PS(R0, 256 + s * SB, SB), pairs), [SB] * len(pairs), rd=["b2", "bn", t("dd", s), t("da", s)], wr=[t("D", s)], bank=[R0], name="D")
+    vec(lambda T, e: e.tensor_scalar(T.pm[:, o:o + n], T["ps%d" % R0][:, 256:256 + n], T.tac[:, e_:e_ + 1], -1.0, OP.is_lt, OP.add), n,
+        rd=[t("D", s) for s in range(NS_)] + [("tac", e_)], wr=[t("pm")], bank=[R0], name="p")
+    pe([mm(PS(R1, 0, n), M("i16"), M("pm", o, n), False, True)], [n], rd=["i16", t("pm")], wr=[t("cn")], bank=[R1], acc=("cn", e_, c), name="cnp")
+    act(M("hd", o, n), PS(R1, 0, n), AF.Relu, n, rd=[t("cn")], wr=[t("hd")], bank=[R1], name="hold")
+    pe(group(PS(R1, 128, n), [(M("i20"), M("pm", o, n)), (M("tri4"), M("hd", o, n))]), [n] * 2, rd=["tri4", "i20", t("hd"), t("pm")], wr=[t("H")], bank=[R1], name="H")
+    vec(lambda T, e: e.tensor_scalar(T.ff[:, o:o + n], T["ps%d" % R1][:, 128:128 + n], 0.0, None, OP.is_equal), n, rd=[t("H")], wr=[t("ff")], bank=[R1], name="f")
+    vec(lambda T, e: e.tensor_tensor(T.mk[:, o:o + n], T.k32[:, o:o + n], T["ps%d" % R1][:, 128:128 + n], OP.min), n, rd=[t("H"), t("k32")], wr=[t("mk")], bank=[R1], name="mk")
+    vec(lambda T, e: e.tensor_copy(T.hl[:, o:o + n], T.mk[:, o:o + n]), n, rd=[t("mk")], wr=[t("hl")], name="hl")
+    if e_ == 0:
+        wrprep(c)
+    vec(lambda T, e: e.tensor_scalar(T.k16[:, o:o + n], T.lst[:, lz:lz + n], -float(PAD), None, OP.add), n, 0.5, rd=[L], wr=[t("k16")], name="k16")
+    add("S", gcost(n), lambda g, T, e: e.activation(T.wg[:, o:o + n], T.wrb[:, 2 * i0:2 * i0 + 2 * n].indirect(T.cl[:, oc:oc + nq]), AF.Copy), rd=[("wrb", c), t("cl")], wr=[t("wg")],
+        name="wg")
+    vec(lambda T, e: e.tensor_tensor(T.dk[:, o:o + n], T.wrb[:, 2 * i0:2 * i0 + 2 * n].indirect(T.cl[:, oc:oc + nq]), T.k32[:, o:o + n], OP.subtract), n, cost=gcost(n),
+        rd=[("wrb", c), t("cl"), t("k32")], wr=[t("dk")], name="dk")
+    vec(lambda T, e: e.tensor_tensor(T.fd[:, o:o + n], T.dk[:, o:o + n], T.ff[:, o:o + n], OP.mult), n, 2, rd=[t("dk"), t("ff")], wr=[t("fd")], name="fd")
+    vec(lambda T, e: e.tensor_tensor(T.va[:, o:o + n], T.k16[:, o:o + n], T.fd[:, o:o + n], OP.add), n, 2, rd=[t("k16"), t("fd")], wr=[t("va")], name="va")
+    pe(group(PS(R0, 0, n), [(M("low"), M("pm", o, n)), (M("i64"), M("ff", o, n))]) + group(PS(R0, n, n), [(M("im64"), M("pm", o, n)), (M("upp"), M("ff", o, n))]),
+       [n] * 4, rd=["low", "i64", "im64", "upp", t("pm"), t("ff")], wr=[t("E")], bank=[R0], name="E")
+    if not last:
+        pe([mm(lambda T: T["ps%d" % R0][0:n, UF:UF + 1], M("ff", o, n), M("one", 0, 1), True, True)], [64], rd=["one", t("ff")], wr=[t("fp")], bank=[R0], name="F1")
+        act(lambda T: T.fs[0:n, e_ * NCH + c:e_ * NCH + c + 1], lambda T: T["ps%d" % R0][0:n, UF:UF + 1], AF.Copy, 1, rd=[t("fp")], wr=[("fs", e_, c)], bank=[R0], name="fs")
+        if c == NCH - 1:
+            count(add, vcost, pcost, e_)
+    act(M("rr", 2 * o, 2 * n), PS(R0, 0, 2 * n), AF.Relu, 2 * n, bias=lambda T: T.c64[:, 0:1], rd=[t("E"), "c64"], wr=[t("rr")], bank=[R0], name="R")
+    pe(group(PS(R0, 256, n), [(M("upp"), M("pm", o, n)), (M("upm"), M("ff", o, n)), (M("idn"), M("rr", 2 * o, n)), (M("idn"), M("rr", 2 * o + n, n))]),
+       [n] * 4, rd=["upp", "upm", "idn", t("pm"), t("ff"), t("rr")], wr=[t("po0")], bank=[R0], name="POS")
+    act(M("po", o, n), PS(R0, 256, n), AF.Identity, n, bias=lambda T: T.c15[:, 0:1], rd=[t("po0"), "c15"], wr=[t("po")], bank=[R0], name="po")
+    for s in range(NS_):
+        a = of + s * SB * 16
+        w = SB * 16
+        add("S", gcost(w), lambda g, T, e, a=a, w=w, s=s: e.activation(T.xh[:, a:a + w], T.gearb[:, 0:PAD + VX].indirect(T.hl[:, o + s * SB:o + s * SB + SB]), AF.Copy),
+            rd=["gearb", "gpad", t("hl")], wr=[t("xh", s)], name="xh")
+        vec(lambda T, e, a=a, w=w: e.tensor_tensor_scan(T.xs[:, a:a + w], T.rst[:, 0:w], T.xh[:, a:a + w], 0.0, OP.mult, OP.max), w, 0.5, rd=["rst", t("xh", s)], wr=[t("xs", s)], name="scan")
+    pe(group(PS(R0, 384, n), [(M("idn"), M("zb", lz, n)), (M("idm"), Sx("xs", of + 15, of + 16 * n, 16))]), [n] * 2, rd=["idn", "idm", Z] + [t("xs", s) for s in range(NS_)],
+       wr=[t("zn")], bank=[R0], name="ZN")
+    zo = e_ * C + i0
+    act(M("zsend", zo, n), PS(R0, 384, n), AF.Abs, n, rd=[t("zn")], wr=[("zsend", e_, c)], bank=[R0], name="z'")
+    for j in range(NB):
+        b = (X0, X1)[j % 2]
+        ms, cols = [], []
+        for kk in range(KB):
+            k = j * KB + kk
+            ms += group(PS(b, kk * n, n), [(M("bp", 128 * k), M("po", o, n)), (M("bk", 128 * k), M("va", o, n))])
+            cols += [n, n]
+        pe(ms, cols, rd=BP + ["bk", t("po"), t("va")], wr=[t("cd", j)], bank=[b], name="cd")
+        a = of + j * 512
+        vec(lambda T, e, a=a, b=b: e.tensor_scalar(T.kl[:, a:a + 512], T["ps%d" % b][:, 0:512], 0.0, 2048.0, OP.max, OP.min), 512, rd=[t("cd", j)], wr=[t("kl", j)], bank=[b], name="clamp")
+        pe([mm(PS(R1, 256, n), M("idn"), M("kl", of + k * n, n), k == 0, k == 15) for k in range(j * KB, j * KB + KB)], [n] * KB, rd=["idn", t("kl", j)],
+           wr=[t("nm") if j == NB - 1 else t("nm", j)], bank=[R1], acc=("nm", e_, c), name="NM")
+    vec(lambda T, e: e.tensor_tensor(T.wrb[:, 2 * i0:2 * i0 + 2 * n].indirect(T.cl[:, oc:oc + nq]), T.wg[:, o:o + n], T.fd[:, o:o + n], OP.subtract), n, cost=0.05 + n * CFG["sc"] * cy,
+        rd=[t("cl"), t("wg"), t("fd")], wr=[("wrb", c)], name="scat")
+    if not last:
+        vec(lambda T, e: e.tensor_scalar(T.lsend[:, zo:zo + n], T["ps%d" % R1][:, 256:256 + n], T.cnm[:, 0:1], None, OP.add), n, rd=[t("nm"), "cnm"], wr=[("lsend", e_, c)],
+            bank=[R1], name="K'")
+        for kind, src, dst in (("z", "zsend", "zb"), ("k", "lsend", "lst")):
+            add("G", 0.3, lambda g, T, e, src=src, dst=dst, kind=kind: (g, T[dst][:, zo + C:zo + C + n], T[src][:, zo:zo + n], "a%s%d_%d" % (kind, e_ + 1, c)),
+                rd=[(src, e_, c)], wr=[(dst, e_ + 1, c)], name="send" + kind, lat=CFG["net"], sem="a%s%d_%d" % (kind, e_ + 1, c), inc="net")
+    else:
+        vec(lambda T, e: e.tensor_scalar(T.yks[:, i0:i0 + n], T["ps%d" % R1][:, 256:256 + n], T.cny[:, 0:1], None, OP.add), n, rd=[t("nm"), "cny"], wr=[("yks", c)],
+            bank=[R1], name="yk")
+        act(M("yws", 2 * i0, 2 * n), M("wrb", 2 * i0, 2 * n), AF.Copy, 2 * n, bias=-float(PAD), rd=[("wrb", c)], wr=[("yws", c)], name="yw")
+        for q, (dst, src, tok, a, b, sa) in enumerate((("yz", "zsend", ("zsend", e_, c), i0, i0 + n, zo), ("yw", "yws", ("yws", c), 2 * i0, 2 * i0 + 2 * n, 2 * i0),
+                                                 ("yk", "yks", ("yks", c), i0, i0 + n, i0))):
+            add("D", 0.0, lambda g, T, e, dst=dst, src=src, a=a, b=b, sa=sa: e.dma_start(T[dst][:, a:b], T[src][:, sa:sa + b - a]), rd=[tok], wr=[(dst, c)], name="store " + dst, lat=2.0,
+                sem="st%d" % (3 * c + q), inc=16)
+
+
+def depend(ops):
+    wrote, readers, banks, last = {}, {}, {}, {}
+    for i, op in enumerate(ops):
+        d = set()
+        for k in op["rd"]:
+            if k in wrote:
+                d.add(wrote[k])
+        for k in op["wr"]:
+            if k in wrote:
+                d.add(wrote[k])
+            d |= readers.get(k, set())
+        for b in op["bank"]:
+            h = banks.setdefault(b, [])
+            for j in h[-40:]:
+                if ops[j]["e"] != op["e"]:
+                    d.add(j)
+            h.append(i)
+        for k in op["rd"]:
+            readers.setdefault(k, set()).add(i)
+        for k in op["wr"]:
+            wrote[k] = i
+            readers[k] = set()
+        d.discard(i)
+        op["dep"] = d
+        op["ord"] = set()
+        if op["acc"] is not None:
+            if op["acc"] in last:
+                op["ord"].add(last[op["acc"]])
+                d.discard(last[op["acc"]])
+            last[op["acc"]] = i
+
+
+def order(ops):
+    N_ = len(ops)
+    succ = [[] for _ in range(N_)]
+    for i, op in enumerate(ops):
+        for j in op["dep"] | op["ord"]:
+            succ[j].append(i)
+    prio = [0.0] * N_
+    for i in range(N_ - 1, -1, -1):
+        prio[i] = ops[i]["dur"] + ops[i]["lat"] + max([prio[j] + CFG["wake"] for j in succ[i]] or [0.0])
+    for i in range(N_):
+        prio[i] += BIAS.get((ops[i]["name"], ops[i]["lc"][1]), 0.0)
+    free, done, left = {}, [0.0] * N_, [len(op["dep"] | op["ord"]) for op in ops]
+    phys = {"E": "S"}
+    ready = {}
+    rt = [0.0] * N_
+    for i in range(N_):
+        if left[i] == 0:
+            ready.setdefault(phys.get(ops[i]["e"], ops[i]["e"]), []).append(i)
+    seq = []
+    while len(seq) < N_:
+        best = None
+        for q, lst in ready.items():
+            if not lst:
+                continue
+            f = free.get(q, 0.0)
+            m = min(max(f, rt[i]) for i in lst)
+            if best is None or m < best[0]:
+                best = (m, q)
+        m, q = best
+        cand = [i for i in ready[q] if max(free.get(q, 0.0), rt[i]) <= m + 1e-9]
+        i = max(cand, key=lambda x: prio[x])
+        ready[q].remove(i)
+        op = ops[i]
+        end = m + op["dur"]
+        free[q] = end
+        op["start"] = m
+        done[i] = end + op["lat"]
+        seq.append(i)
+        for j in succ[i]:
+            left[j] -= 1
+            rt[j] = max(rt[j], done[i] + CFG["wake"])
+            if left[j] == 0:
+                ready.setdefault(phys.get(ops[j]["e"], ops[j]["e"]), []).append(j)
+    return seq, max(done)
+
+
+def plan():
+    if "p" not in CACHE:
+        ops = build()
+        depend(ops)
+        seq, span = order(ops)
+        cnt = {}
+        know = {}
+        clock = {}
+        steps = []
+        for i in seq:
+            op = ops[i]
+            q = {"E": "S"}.get(op["e"], op["e"])
+            kn = know.setdefault(q, {})
+            waits = {}
+            for j in sorted(op["dep"], key=lambda x: -ops[x]["pos"]):
+                s, v = ops[j]["at"]
+                if kn.get(s, 0) < v:
+                    waits[s] = max(waits.get(s, 0), v)
+                    for s2, v2 in clock[j].items():
+                        kn[s2] = max(kn.get(s2, 0), v2)
+            op["pos"] = len(steps)
+            if op["sem"] is None:
+                s = {"V": "sV", "S": "sS", "P": "sP", "G": "sG"}[op["e"]]
+                cnt[s] = cnt.get(s, 0) + 1
+                op["at"] = (s, cnt[s])
+            else:
+                op["at"] = (op["sem"], op["inc"] if op["inc"] != "net" else 1)
+            clock[i] = dict(kn) if op["inc"] != "net" else {}
+            clock[i][op["at"][0]] = op["at"][1]
+            steps.append((op, sorted(waits.items())))
+        CACHE["p"] = (steps, cnt, span)
+    return CACHE["p"]
+
+
+def rank_program(g, core, T, topo):
+    rank = T.rank_of(core)
+    if rank is None:
+        return
+    nxt = T.cores[(rank + 1) % len(T.cores)]
+    prv = T.cores[(rank - 1) % len(T.cores)]
+    rid, pid, _se = topo.addr(nxt)
+    eng = topo.engines(core, nxt)[:8]
+    neng_in = len(topo.engines(prv, core)[:8])
+    emask = 0
+    for x in eng:
+        emask |= 1 << x
+    queues = {"V": g.vector, "S": g.scalar, "P": g.tensor, "G": g, "D": g.sync, "E": g.scalar}
+    steps, cnt, span = plan()
+    sent = 0
+    for op, waits in steps:
+        q = queues[op["e"]]
+        for s, v in waits:
+            q.wait_ge(T.sem[s], neng_in if s[0] == "a" else v)
+        if op["inc"] == "net":
+            _g, out, in_, rs = op["fn"](g, T, q)
+            g.remote_dma(out, in_, T.sem[rs], T.sem.sent, pid, rid, emask)
+            sent += len(eng)
+        else:
+            r = op["fn"](g, T, q)
+            if op["sem"] is None:
+                r.then_inc(T.sem[op["at"][0]], 1)
+            else:
+                r.then_inc(T.sem[op["sem"]], 16)
+    for s, v in sorted(cnt.items()):
+        g.wait_ge(T.sem[s], v)
+    g.wait_ge(T.sem.sent, sent)
+    for k in LOADS:
+        g.wait_ge(T.sem["ld_" + k], 16)
+    for k in range(3 * NCH):
+        g.wait_ge(T.sem["st%d" % k], 16)

@@ -4,58 +4,72 @@ from concourse.mybir import dt, AluOpType as OP, AxisListType, ActivationFunctio
 VX, VY, C, LE = 2048, 4096, 256, 5
 NCH = 2
 n = C // NCH
-SB = 64
-NS_ = n // SB
+XG = (32, 32, 32, 32)
+XB = (32, 32, 64)
 nq = n // 16
-PAD = 32
 KB = 512 // n
 NB = 16 // KB
-ABS_S = (0,)
-CFG = {"fix": {"V": 0.03, "S": 0.05, "P": 0.0, "G": 0.05, "D": 0.06, "E": 0.06}, "pe": 0.417e-3, "cy": 0.83e-3 * 1.25, "ga": 1.56,
-       "sc": 3.8, "wake": 0.08, "net": 2.6, "jit": 0.0}
-
-
-UF = 256
+RELU_V = {(0, 2), (1, 2)}
+HELD1 = 4
+PICK = (("S", 3), ("S", 3), ("S", 2))
+UMOD = True
+ESPLIT = False
+CDX = 0
+XMX = 1
+POS2 = False
+ROUND = """
+xp3 D0 D p wrb ta> scat> cnt2 cnt3 <U0 cnp <UL stop dk <ci <uh N0 N nfh xp1 xp xm <v5 sendk> <k32 <x1 <vv E R xm1 <bi <U37 f POS <cc xp2 scan scan1
+xm3 <cl mult <x a s <P v <T <x2 scan3 xm2 <T2 cd pick <x3 scan2 cd1 pick1 cd2 pick2 <SL NM mm ZN z' st_yz st_yw> <y <y1 sendz <xz <sg <sg1 NM1 NM2
+<xz1 ui <sg2 <sg3 uj K' <y2 <k16 <cnt <abs1 <relu F2 fi <abs <xz2 <sg4 w' yk st_yk <sg5 <xz3 <sg6 <sg7 <cnt1 fm
+"""
+START = """
+one rsc1 m64 d0a_1 d0b_0 d0a_0 rst1 kf k15 ld_z0 ld_wt cz wcol |U0:0 rsc idn tmpa iq idm im16 i16 ta tb tmpb blkm ld_rk lst0 b1 bw k8 rst cb1 lw
+ta_128 cj wa |ci:0 icq io1 io2 |uh:0 s1 wac |bi:0 wb |U37:0 ck2 |cl:0 lwa ld_gx lwb tb_128 ld_rt ld_sy ld_th |P:0 one32 lst01 |T:0 d1 |x2:0 im2 |x3:0
+j1 s3 j2 s6 cub j3 |SL:0 ih i32 oth |y:0 s4 |y1:0 ct ld_wr |xz:0 tdg s5 |k16:0 low lowh s41 |sg5:0 upp |xz3:0 s61 |U0:1 m1h |cnp:0 m1f m2f bkh wn bkh1
+own bo |stop:0 bo1 bo2 bo3 bo4 bap |N0:0 cs |v5:1 ca |k32:1 uph bo5 |E:0 bo6 bo7 bap1 |U37:1 ba |f:0 bs |scan1:0 ba1 |cl:1
+"""
+CFG = {"fix": {"V": 0.03, "S": 0.05, "P": 0.0, "G": 0.05, "D": 0.06, "E": 0.06}, "pe": 0.417e-3 * 1.15, "cy": 0.83e-3 * 1.15, "ga": 1.56,
+       "sc": 3.8, "wake": 0.08, "net": 2.6, "T": 20.0, "gap": 1.0, "look": 0.4}
 FB = 4 * ((NCH - 1) % 2)
 CUR = {"lc": (0, 0)}
 CACHE = {}
-BIAS = {("UL", 0): -17.0, ("x", 0): 5.0, ("xz", 0): -1.9, ("sg", 0): 15.0, ("cnt", 0): -12.2, ("y", 0): 40.4, ("abs", 0): -0.9, ("D", 0): 14.1, ("relu", 0): 39.5,
-        ("mk", 0): 6.4, ("wg", 0): 8.4, ("dk", 0): -4.9, ("va", 0): -20.3, ("E", 0): 7.3, ("xh", 0): -24.3, ("scan", 0): -0.8, ("clamp", 0): 0.6, ("NM", 0): -24.8,
-        ("scat", 0): 17.4, ("K'", 0): -3.6, ("UL", 1): 1.8, ("D", 1): -5.6, ("scan", 1): -10.1, ("R", 1): 3.3, ("relu", 1): -7.6, ("scat", 1): 1.1, ("E", 1): -7.5,
-        ("va", 1): -1.1, ("z'", 1): 10.5, ("fd", 1): -11.2, ("P", 1): 16.2, ("cd", 1): 3.7, ("K'", 1): 8.0, ("NM", 1): 0.5, ("abs", 1): -6.7, ("cnt", 1): -2.0,
-        ("dk", 1): -7.1, ("sg", 1): 6.2, ("wg", 1): -1.7, ("x", 1): -6.6, ("xz", 1): 6.9}
-
-
-def two(name, dtype, cols):
-    return {name: ("sbuf", [128, cols], dtype)}
-
+BIAS = {("nfh", 1): -6, ("scan", 0): 1.3, ("w'", 0): -18, ("y", 0): -1.4, ("Q", 1): -6, ("a", 0): 3, ("xm", 0): -1, ("k32", 1): -9, ("k16", 0): -11.4,
+        ("Q", 0): 4.7, ("abs", 0): -2, ("stop", 0): -1, ("F2", 1): -14, ("cl", 0): -6, ("k16", 1): -4, ("cd", 0): 2, ("ZN", 0): 20, ("mm", 0): 8,
+        ("wrb", 1): -11, ("dk", 0): -8, ("NM", 0): 2, ("D", 0): -4, ("yk", 0): -13, ("wrb", 0): 2, ("T", 1): 3, ("POS", 1): 5, ("E", 1): 4,
+        ("scan", 1): 0.4, ("mult", 0): 2}
 
 SCRATCH = {}
 for _nm, _dt, _co in (
-        ("gearb", "bfloat16", PAD + VX), ("siteb", "bfloat16", VY), ("rkb", "int32", C), ("rtb", "int32", 2 * C), ("wri", "int32", 2 * C),
-        ("wrb", "float32", 2 * C), ("wtb", "bfloat16", 2), ("thb", "int32", 2), ("tcol", "float32", 2), ("tac", "float32", 8),
+        ("gearb", "bfloat16", VX), ("siteb", "bfloat16", VY), ("rkb", "int32", C), ("rtb", "int32", 2 * C), ("wri", "int32", 2 * C),
+        ("wrb", "float32", 2 * C), ("wtb", "bfloat16", 2), ("thb", "int32", 2), ("tac", "float32", 8),
         ("lst", "uint16", LE * C), ("lsend", "uint16", LE * C), ("zb", "bfloat16", LE * C), ("zsend", "bfloat16", LE * C),
         ("ci", "int32", 2 * NCH * nq), ("v5", "int32", 2 * NCH * nq), ("vv", "int32", 2 * NCH * nq), ("bi", "int32", 2 * NCH * nq),
         ("cc", "int32", 2 * NCH * nq), ("cl", "uint16", 2 * C),
-        ("k32", "float32", 2 * C), ("k16", "float16", 2 * C), ("pp", "int32", 2 * C), ("qq", "int32", 2 * C), ("tt", "int32", 2 * C),
+        ("k32", "float32", 2 * C), ("pp", "int32", 2 * C), ("qq", "int32", 2 * C), ("tt", "int32", 2 * C),
         ("t2", "int32", 2 * C), ("sl", "uint16", 2 * C),
         ("xx", "bfloat16", 32 * C), ("dd", "bfloat16", 32 * C), ("da", "bfloat16", 32 * C), ("sg", "bfloat16", 32 * C),
-        ("pm", "bfloat16", 2 * C), ("hd", "bfloat16", 2 * C), ("ff", "bfloat16", 2 * C), ("mk", "float32", 2 * C), ("hl", "uint16", 2 * C),
-        ("xh", "bfloat16", 32 * C), ("xs", "bfloat16", 32 * C), ("rr", "bfloat16", 4 * C), ("po", "bfloat16", 2 * C),
-        ("wg", "float32", 2 * C), ("dk", "float32", 2 * C), ("fd", "float32", 2 * C), ("va", "float16", 2 * C), ("kl", "float16", 32 * C),
-        ("yks", "float32", C), ("yws", "float32", 2 * C),
-        ("fs", "bfloat16", LE * NCH), ("fi", "int32", LE), ("fm", "int32", LE),
-        ("one", "bfloat16", 2048), ("b1", "bfloat16", 144), ("b2", "bfloat16", 144), ("bn", "bfloat16", 144), ("bh", "bfloat16", 144),
-        ("bw", "bfloat16", 144), ("tmpa", "bfloat16", 144), ("tmpb", "bfloat16", 144), ("tmpc", "bfloat16", 128),
-        ("blk", "bfloat16", 128), ("idn", "bfloat16", 128), ("idm", "bfloat16", 128), ("i16", "bfloat16", 128), ("i20", "bfloat16", 128),
-        ("i64", "bfloat16", 128), ("im64", "bfloat16", 128), ("i384", "bfloat16", 128),
-        ("tri", "bfloat16", 128), ("tri4", "bfloat16", 128), ("low", "bfloat16", 128), ("upp", "bfloat16", 128), ("upm", "bfloat16", 128),
-        ("bk", "bfloat16", 2048), ("bp", "bfloat16", 2048), ("mb0", "bfloat16", 128), ("mb1", "bfloat16", 128),
+        ("pm", "bfloat16", 2 * C), ("sv", "bfloat16", 2 * C), ("rr", "bfloat16", 4 * C), ("aa", "bfloat16", 2 * C), ("ss", "bfloat16", 2 * C),
+        ("d0a", "bfloat16", 6 * C), ("d0b", "bfloat16", 3 * C), ("d1", "float16", 3 * C), ("oa", "float16", 6 * C), ("ob", "float16", 6 * C),
+        ("xs", "float16", 32 * C), ("mm", "float16", 2 * C), ("kl", "float16", 16 * C), ("ui", "int32", 2 * C), ("uj", "int32", 2 * C),
+        ("yks", "float32", C), ("fs", "float32", LE * NCH), ("fi", "int32", LE), ("fm", "int32", LE),
+        ("one", "bfloat16", 144), ("one32", "float32", 128), ("m64", "bfloat16", 2048), ("b1", "bfloat16", 144),
+        ("bw", "bfloat16", 144), ("tmpa", "bfloat16", 144), ("tmpb", "bfloat16", 144), ("blkm", "bfloat16", 128),
+        ("idn", "bfloat16", 128), ("idm", "bfloat16", 128), ("i16", "bfloat16", 128), ("im16", "bfloat16", 128), ("i32", "bfloat16", 128),
+        ("ih", "bfloat16", 128), ("im2", "bfloat16", 128), ("im32", "bfloat16", 128), ("lowh", "bfloat16", 128), ("lw", "bfloat16", 128),
+        ("iq", "bfloat16", 128), ("icq", "bfloat16", 128), ("uh", "bfloat16", 2 * C),
+        ("ta", "bfloat16", 256), ("tb", "bfloat16", 256), ("tdg", "float16", 128),
+        ("low", "bfloat16", 128), ("upp", "bfloat16", 128), ("m1f", "bfloat16", 128), ("m1h", "bfloat16", 128), ("m2f", "bfloat16", 128),
+        ("uph", "bfloat16", 128), ("s1", "bfloat16", 128), ("s2", "bfloat16", 128), ("s3", "bfloat16", 128), ("s4", "bfloat16", 128),
+        ("s5", "bfloat16", 128), ("s6", "bfloat16", 128), ("j1", "bfloat16", 128), ("j2", "bfloat16", 128), ("j3", "bfloat16", 128),
+        ("own", "bfloat16", 128), ("oth", "bfloat16", 128), ("wn", "bfloat16", 128),
+        ("bkh", "bfloat16", 2048), ("bs", "bfloat16", 1024), ("bo", "bfloat16", 1024), ("ba", "float16", 1024),
         ("w37", "float32", 2), ("wa", "bfloat16", 2), ("wb", "float32", 2), ("wac", "float32", 2), ("wcol", "float32", 2),
         ("lwa", "bfloat16", 128), ("lwb", "bfloat16", 128),
-        ("rst", "bfloat16", 16 * n), ("io2", "int32", nq), ("kf", "float32", 2), ("cz", "float32", 8),
-        ("c64", "float32", 2), ("c15", "float32", 2), ("cnm", "float32", 2), ("cny", "float32", 2)):
-    SCRATCH.update(two(_nm, _dt, _co))
+        ("rst", "float16", 512), ("rsc", "bfloat16", 128), ("io1", "int32", nq), ("io2", "int32", nq), ("kf", "int32", 2), ("k15", "int32", 2),
+        ("cz", "float32", 2), ("k8", "int32", 2),
+        ("ct", "float32", 2), ("cr", "float32", 2), ("ca", "float32", 2), ("cs", "float32", 2), ("ck2", "float32", 2), ("cb1", "float32", 2),
+        ("cub", "float32", 2), ("cj", "float32", 2)):
+    SCRATCH[_nm] = ("sbuf", [128, _co], _dt)
 for _b in range(8):
     SCRATCH["ps%d" % _b] = ("psum", [128, 512], "float32")
 
@@ -64,158 +78,211 @@ SEMAPHORES = ["sV", "sS", "sP", "sG", "sent"] + ["ld_" + x for x in LOADS] + ["s
 SEMAPHORES += ["a%s%d_%d" % (k, e, c) for k in "kz" for e in range(1, LE) for c in range(NCH)]
 
 
-def sl(T, name, a, b, st=1):
-    return T[name][:, a:b] if st == 1 else T[name][:, a:b:st]
+def cost(op, cfg):
+    kind, m = op["c"]
+    cy = cfg["cy"]
+    d = {"v": lambda: max(64, m) * cy, "g": lambda: 0.03 + m * cfg["ga"] * cy, "s": lambda: 0.03 + m * cfg["sc"] * cy,
+         "p": lambda: sum(max(64, x) for x in m) * cfg["pe"], "G": lambda: 0.15 + 2 * m * cy, "net": lambda: 0.3, "dma": lambda: 0.0}[kind]()
+    return d + cfg["fix"][op["e"]], cfg["net"] if kind == "net" else (m if kind == "dma" else 0.0)
+
+
+def M(nm, a=0, w=128, st=1):
+    if st == 1:
+        return lambda T: T[nm][:, a:a + w]
+    return lambda T: T[nm][:, a:a + st * (w - 1) + 1:st]
+
+
+def REV(nm, a, w):
+    return lambda T: T[nm][:, a + w - 1:(a - 1 if a else None):-1]
+
+
+def PS(b, a, w, st=1):
+    return M("ps%d" % b, a, w, st)
+
+
+def col(nm):
+    return M(nm, 0, 1)
+
+
+def at(x, T):
+    return x if isinstance(x, (int, float)) or x is None else x(T)
+
+
+def tools(add):
+    def vec(f, m, kind="v", **kw):
+        add("V", (kind, m), lambda g, T, e: f(T, e), **kw)
+
+    def ts(out, src, s1, s2, o1, o2, m, **kw):
+        if o2 is None:
+            vec(lambda T, e: e.tensor_scalar(out(T), src(T), at(s1, T), None, o1), m, **kw)
+        else:
+            vec(lambda T, e: e.tensor_scalar(out(T), src(T), at(s1, T), at(s2, T), o1, o2), m, **kw)
+
+    def tt(out, a, b, op, m, **kw):
+        vec(lambda T, e: e.tensor_tensor(out(T), a(T), b(T), op), m, **kw)
+
+    def cp(out, src, m, **kw):
+        vec(lambda T, e: e.tensor_copy(out(T), src(T)), m, **kw)
+
+    def scan(out, d0, d1, first, o0, o1, m, **kw):
+        vec(lambda T, e: e.tensor_tensor_scan(out(T), d0(T), d1(T), first, o0, o1), m, **kw)
+
+    def act(out, src, func, m, bias=None, scale=None, acc_out=None, kind="v", **kw):
+        def f(g, T, e):
+            k = {}
+            if bias is not None:
+                k["bias"] = at(bias, T)
+            if scale is not None:
+                k["scale"] = at(scale, T)
+            if acc_out is not None:
+                k["accum_out"] = acc_out(T)
+            return e.activation(out(T), src(T), func, **k)
+        add("S", (kind, m), f, **kw)
+
+    def pe(mms, **kw):
+        def f(g, T, e):
+            for o, l, r, s0, s1, _c in mms:
+                x = e.matmul(o(T), l(T), r(T), s0, s1)
+            return x
+        add("P", ("p", [m[5] for m in mms]), f, **kw)
+
+    def group(out, pairs, cols):
+        return [(out, l, r, i == 0, i == len(pairs) - 1, cols) for i, (l, r) in enumerate(pairs)]
+    return vec, ts, tt, cp, scan, act, pe, group
 
 
 def build():
     ops = []
-    cy, ga, fix = CFG["cy"], CFG["ga"], CFG["fix"]
+    CUR["lc"] = (-1, 0)
 
-    def add(eng, cost, fn, rd=(), wr=(), bank=(), name="", lat=0.0, sem=None, inc=1, acc=None):
-        ops.append({"e": eng, "dur": cost + fix[eng], "fn": fn, "rd": list(rd), "wr": list(wr), "bank": list(bank), "name": name,
-                    "lat": lat, "sem": sem, "inc": inc, "lc": CUR["lc"], "acc": acc})
+    def add(eng, c, fn, rd=(), wr=(), bank=(), name="", sem=None, inc=1, acc=None):
+        op = {"e": eng, "c": c, "fn": fn, "rd": list(rd), "wr": list(wr), "bank": list(bank), "name": name or str(wr[0]),
+              "sem": sem, "inc": inc, "lc": CUR["lc"], "acc": acc, "id": len(ops)}
+        op["dur"], op["lat"] = cost(op, CFG)
+        ops.append(op)
+    vec, ts, tt, cp, scan, act, pe, group = tools(add)
 
-    def vcost(m, cyc=1.0):
-        return max(64, m * cyc) * cy
+    def load(q, dst, src, w, key, lat):
+        add(q, ("dma", lat), lambda g, T, e: e.dma_start(T[dst][:, 0:w], T[src][:]), wr=[dst] if dst != "zb" else [("zb", 0, c) for c in range(NCH)],
+            name="load " + src, sem="ld_" + key, inc=16, acc=("load", q))
+    load("D", "rkb", "rk", C, "rk", 2.0)
+    load("E", "zb", "z0", C, "z", 2.0)
+    load("E", "wtb", "wt", 1, "wt", 2.0)
+    load("D", "gearb", "gx", VX, "gear", 3.6)
+    load("D", "rtb", "rt", 2 * C, "rt", 4.3)
+    load("D", "siteb", "sy", VY, "site", 7.0)
+    load("D", "thb", "th", 1, "th", 7.0)
+    load("D", "wri", "wr", 2 * C, "wr", 7.7)
 
-    def gcost(m):
-        return 0.04 + m * ga * cy
-
-    def pcost(*cols):
-        return sum(max(64, x) for x in cols) * CFG["pe"] * 1.25
-
-    def load(q, dst, src, a, b, key, lat):
-        add(q, 0.0, lambda g, T, e: e.dma_start(sl(T, dst, a, b), T[src][:]), wr=[dst] if dst != "zb" else [("zb", 0, c) for c in range(NCH)],
-            name="load " + src, lat=lat, sem="ld_" + key, inc=16)
-    load("D", "wtb", "wt", 0, 1, "wt", 2.0)
-    load("E", "zb", "z0", 0, C, "z", 2.0)
-    load("D", "rkb", "rk", 0, C, "rk", 2.2)
-    load("D", "gearb", "gx", PAD, PAD + VX, "gear", 4.5)
-    load("E", "rtb", "rt", 0, 2 * C, "rt", 3.5)
-    load("E", "thb", "th", 0, 1, "th", 4.0)
-    load("D", "siteb", "sy", 0, VY, "site", 8.0)
-    load("E", "wri", "wr", 0, 2 * C, "wr", 4.0)
-
-    def aff(dst, src, m, pat, cmp_, base, cm, w=None):
-        add("G", 0.17 + 2 * m * cy, lambda g, T, e: e.affine_select(sl(T, dst, 0, m), sl(T, src, 0, m), pat, cmp_, 0.0, base, cm),
-            rd=[src], wr=[dst], name="aff " + dst)
+    def aff(dst, src, m, pat, cmp_, base, cm, a=0, other=0.0):
+        add("G", ("G", m), lambda g, T, e: e.affine_select(T[dst][:, a:a + m], T[src][:, 0:m], pat, cmp_, other, base, cm),
+            rd=[src], wr=[dst if a == 0 else (dst, a)], name="aff " + dst, acc="G")
 
     def iot(dst, m, pat, base, cm):
         def f(g, T, e):
             if SCRATCH[dst][2] == "int32":
-                return e.iota(sl(T, dst, 0, m), pat, base, cm)
-            return e.iota(sl(T, dst, 0, m), pat, base, cm, allow_small_or_imprecise_dtypes=True)
-        add("G", 0.13 + 2 * m * cy, f, wr=[dst], name="iota " + dst)
+                return e.iota(T[dst][:, 0:m], pat, base, cm)
+            return e.iota(T[dst][:, 0:m], pat, base, cm, allow_small_or_imprecise_dtypes=True)
+        add("G", ("G", m), f, wr=[dst], name="iota " + dst, acc="G")
 
-    def ts(dst, a, b, src, c0, d, s1, s2, o1, o2=None, rd=None, wr=None, cyc=1.0, bank=(), eng="V", st=1, sst=1, dst_st=1):
-        def f(g, T, e):
-            x1 = s1(T) if callable_(s1) else s1
-            x2 = s2(T) if callable_(s2) else s2
-            if o2 is None:
-                return e.tensor_scalar(sl(T, dst, a, b, dst_st), sl(T, src, c0, d, sst), x1, None, o1)
-            return e.tensor_scalar(sl(T, dst, a, b, dst_st), sl(T, src, c0, d, sst), x1, x2, o1, o2)
-        add("V", vcost((b - a) // dst_st, cyc), f, rd=rd, wr=wr, bank=bank, name="ts " + dst)
+    def fill(dst, ap, v, m, rd=(), wr=None):
+        vec(lambda T, e: e.memset(ap(T), v), m, rd=rd, wr=wr or [dst])
 
-    def callable_(x):
-        return not isinstance(x, (int, float)) and x is not None
+    def cst(dst, src, m, mul, addv=None, a=0, rd=()):
+        ts(M(dst, a, m), M(src, 0, m), mul, addv, OP.mult, None if addv is None else OP.add, m // 2, rd=[src] + list(rd), wr=[dst if a == 0 else (dst, a)])
 
-    def cst(dst, src, m, mul, addv=None):
-        if addv is None:
-            ts(dst, 0, m, src, 0, m, mul, None, OP.mult, rd=[src], wr=[dst], cyc=0.5)
-        else:
-            ts(dst, 0, m, src, 0, m, mul, addv, OP.mult, OP.add, rd=[src], wr=[dst])
+    def sca(dst, src, m, mul, addv=None, a=0, rd=()):
+        act(M(dst, a, m), M(src, 0, m), AF.Copy, m, bias=addv, scale=mul, rd=[src] + list(rd), wr=[dst if a == 0 else (dst, a)])
 
-    add("V", 0.3, lambda g, T, e: e.memset(T.one[:, 0:144], 1.0), wr=["one"], name="one")
-    add("V", vcost(32), lambda g, T, e: e.memset(T.gearb[:, 0:PAD], 0.0), wr=["gpad"], name="gpad")
+    fill("one", M("one", 0, 144), 1.0, 72)
+    fill("m64", M("m64", 0, 1024), -64.0, 512)
+    iot("kf", 1, [[0, 1]], 0, 1)
+    aff("idn", "one", 128, [[-1, 128]], OP.is_equal, 0, 1)
     aff("tmpa", "one", 144, [[-16, 9], [0, 16]], OP.is_ge, 0, 1)
     aff("tmpb", "tmpa", 144, [[16, 9], [0, 16]], OP.is_ge, 15, -1)
     aff("b1", "tmpb", 144, [[0, 9], [1, 16]], OP.is_equal, -15, 0)
-    ts("wcol", 0, 1, "wtb", 0, 1, 1.0, None, OP.mult, rd=["wtb"], wr=["wcol"])
-    add("V", vcost(144, .5), lambda g, T, e: e.tensor_scalar(T.bw[:, 0:144], T.b1[:, 0:144], T.wcol[:, 0:1], None, OP.mult), rd=["b1", "wcol"], wr=["bw"], name="bw")
-    iot("io2", nq, [[32, nq]], 0, 0)
-    iot("kf", 1, [[0, 1]], 0, 1)
-    ts("w37", 0, 1, "wtb", 0, 1, 37.0, None, OP.mult, rd=["wtb"], wr=["w37"])
-    ts("wa", 0, 1, "w37", 0, 1, 1.0, None, OP.mult, rd=["w37"], wr=["wa"])
-    ts("wac", 0, 1, "wa", 0, 1, 1.0, None, OP.mult, rd=["wa"], wr=["wac"])
-    add("V", vcost(1), lambda g, T, e: e.tensor_tensor(T.wb[:, 0:1], T.w37[:, 0:1], T.wac[:, 0:1], OP.subtract), rd=["w37", "wac"], wr=["wb"], name="wb")
-    add("V", vcost(128, .5), lambda g, T, e: e.tensor_scalar(T.lwa[:, 0:128], T.tmpb[:, 0:128], T.wac[:, 0:1], None, OP.mult), rd=["tmpb", "wac"], wr=["lwa"], name="lwa")
-    add("V", vcost(128, .5), lambda g, T, e: e.tensor_scalar(T.lwb[:, 0:128], T.tmpb[:, 0:128], T.wb[:, 0:1], None, OP.mult), rd=["tmpb", "wb"], wr=["lwb"], name="lwb")
-    add("V", vcost(1), lambda g, T, e: e.tensor_copy(T.ci[:, 0:1], T.kf[:, 0:1]), rd=["kf"], wr=[("ci", 0, 0)], name="k0")
-    ts("v5", 0, 1, "ci", 0, 1, 15, None, OP.bitwise_and, rd=[("ci", 0, 0)], wr=[("v5", 0, 0)])
-    ts("cz", 0, 1, "v5", 0, 1, 1.0, None, OP.mult, rd=[("v5", 0, 0)], wr=["cz"])
-    cst("c64", "cz", 1, 1.0, -64.0)
-    cst("c15", "cz", 1, -1.0, 15.0)
-    cst("cny", "cz", 1, 2048.0, -2048.0 * 15)
-    cst("cnm", "cz", 1, 2048.0, -2048.0 * 15 + PAD)
-    add("V", vcost(nq), lambda g, T, e: e.tensor_scalar(T.cc[:, 0:nq], T.io2[:, 0:nq], T.cz[:, 0:1], T.cz[:, 0:1], OP.add, OP.add), rd=["io2", "cz"],
-        wr=[("cc", 0, 0)], name="io2b")
-    add("V", vcost(nq), lambda g, T, e: e.tensor_copy(T.io2[:, 0:nq], T.cc[:, 0:nq]), rd=[("cc", 0, 0)], wr=["io2"], name="io2c")
-    ts("tcol", 0, 1, "thb", 0, 1, 1.0, None, OP.mult, rd=["thb"], wr=["tcol"])
-    ts("tac", 0, 1, "thb", 0, 1, 1.0, None, OP.mult, rd=["thb"], wr=[("tac", 0)])
-    aff("idn", "one", 128, [[-1, 128]], OP.is_equal, 0, 1)
-    cst("idm", "idn", 128, -1.0)
-    cst("i16", "idn", 128, 16.0)
-    cst("bh", "b1", 144, 0.5)
-    cst("b2", "b1", 144, 2.0)
-    cst("bn", "b1", 144, -1.0)
-    aff("tri", "tmpb", 128, [[-1, 128]], OP.is_ge, 0, 1)
-    cst("tri4", "tri", 128, 4096.0)
-    cst("i20", "idn", 128, 1048576.0)
-    aff("low", "tmpb", 128, [[1, 128]], OP.is_ge, -1, -1)
-    aff("upp", "tmpb", 128, [[-1, 128]], OP.is_ge, -1, 1)
-    cst("upm", "upp", 128, -1.0)
-    cst("i64", "idn", 128, 64.0)
-    cst("im64", "idn", 128, -64.0)
-    cst("i384", "idn", 128, 3840.0)
-    iot("mb0", 128, [[0, 8], [-32, 16]], 0, 0)
-    add("V", vcost(128, 2), lambda g, T, e: e.tensor_tensor(T.mb1[:, 0:128], T.mb0[:, 0:128], T.tmpb[:, 0:128], OP.mult), rd=["mb0", "tmpb"], wr=["mb1"], name="mb1")
-    add("V", vcost(2048, .5), lambda g, T, e: e.memset(T.kl[:, 0:16], 0) if False else e.memset(T.rst[:, 0:16 * n], 1.0), wr=["rst1"], name="rst1")
-    aff_src = "rst1"
-    add("G", 0.17 + 2 * 2048 * cy, lambda g, T, e: e.affine_select(T.bk[:, 0:2048], T.rst[:, 0:2048], [[-1, 16], [-16, 8], [0, 16]], OP.is_equal, 0.0, 0, 1),
-        rd=[aff_src, "upp", "low", "tri", "idn"], wr=["bk"], name="bk")
-    add("V", vcost(n), lambda g, T, e: e.memset(T.rst[:, 0:16 * n:16], 0.0), rd=["rst1", "bk"], wr=["rst", "rst1"], name="rst")
-    for j in range(4):
-        b = j + 2 if j < 2 else j + 4
-
-        def fbp(g, T, e, j=j, b=b):
-            ps = T["ps%d" % b]
-            for k in range(4):
-                e.matmul(ps[:, 128 * k:128 * k + 128], T.i384[:, 0:128], T.bk[:, 512 * j + 128 * k:512 * j + 128 * k + 128], True, False)
-                r = e.matmul(ps[:, 128 * k:128 * k + 128], T.idn[:, 0:128], T.mb1[:, 0:128], False, True)
-            return r
-        add("P", pcost(*[128] * 8), fbp, rd=["i384", "bk", "idn", "mb1"], wr=[("bpp", j)], bank=[b], name="bpp")
-        add("S", 512 * cy, lambda g, T, e, j=j, b=b: e.activation(T.bp[:, 512 * j:512 * j + 512], T["ps%d" % b][:, 0:512], AF.Copy), rd=[("bpp", j)], wr=["bp%d" % j],
-            bank=[b], name="bp")
-    BP = ["bp%d" % j for j in range(4)]
+    iot("io1", nq, [[32, nq]], 0, 0)
+    sca("blkm", "tmpb", 128, -1.0)
+    iot("j1", 128, [[0, 16], [2, 8]], 1, 0)
+    iot("s3", 128, [[0, 8], [2, 16]], -15, 0)
+    aff("low", "blkm", 128, [[1, 128]], OP.is_ge, -1, -1)
+    aff("upp", "blkm", 128, [[-1, 128]], OP.is_ge, -1, 1)
+    aff("m1f", "low", 128, [[-1, 128]], OP.not_equal, 0, 1, other=-32.0)
+    aff("m2f", "upp", 128, [[-1, 128]], OP.not_equal, 0, 1, other=64.0)
+    for a in range(2):
+        aff("bkh", "m64", 1024, [[-1, 8], [-16, 8], [0, 16]], OP.is_equal, -8 * a, 1, a=1024 * a)
+    iot("own", 128, [[0, 16], [512, 8]], 384, 0)
+    for t_ in range(8):
+        aff("bo", "own", 128, [[-8, 16], [0, 8]], OP.is_equal, -t_, 1, a=128 * t_)
+    aff("bs", "m64", 1024, [[-1, 8], [-8, 16], [0, 8]], OP.is_equal, 0, 1)
+    ts(col("k15"), col("kf"), 15, None, OP.bitwise_and, None, 1, rd=["kf"], wr=["k15"])
+    ts(col("k8"), col("kf"), 7, None, OP.bitwise_and, None, 1, rd=["kf"], wr=["k8"])
+    cst("cz", "k15", 1, 1.0)
+    cst("cj", "k8", 1, 2.0, 1.0)
+    ts(M("io2", 0, nq), M("io1", 0, nq), col("cz"), col("cz"), OP.add, OP.add, nq, rd=["io1", "cz"], wr=["io2"])
     for c in range(NCH):
-        i0 = c * n
-        ts("lst", i0, i0 + n, "rkb", i0, i0 + n, float(PAD), None, OP.add, rd=["rkb"], wr=[("lst", 0, c)])
-
-    def wrprep(c):
-        ts("wrb", 2 * c * n, 2 * c * n + 2 * n, "wri", 2 * c * n, 2 * c * n + 2 * n, float(PAD), None, OP.add, rd=["wri"], wr=[("wrb", c)])
+        cp(M("lst", c * n, n), M("rkb", c * n, n), n, rd=["rkb"], wr=[("lst", 0, c)], name="lst0")
+    cst("wcol", "wtb", 1, 1.0)
+    cst("bw", "b1", 144, col("wcol"), rd=["wcol"])
+    w37 = 37.0 * 32 if UMOD else 37.0
+    cst("wa", "wtb", 1, w37)
+    cst("wac", "wa", 1, 1.0)
+    ts(col("wb"), col("wtb"), w37, col("wac"), OP.mult, OP.subtract, 1, rd=["wtb", "wac"], wr=["wb"])
+    cst("lwa", "tmpb", 128, col("wac"), rd=["wac"])
+    cst("lwb", "tmpb", 128, col("wb"), rd=["wb"])
+    if UMOD:
+        cst("lw", "tmpb", 128, col("wcol"), rd=["wcol"])
+        sca("iq", "idn", 128, -37.0 * 2 ** 17)
+        sca("icq", "idn", 128, 37.0 * 2 ** 24)
+    for nm, x in (("idm", -1.0), ("im16", -16.0), ("i16", 16.0), ("i32", 32.0), ("ih", 0.5), ("im2", -2.0)):
+        sca(nm, "idn", 128, x)
+    for a, (x, y) in enumerate(((-8.0, 0.5), (-7.5, -0.5))):
+        sca("ta", "idn", 128, x, a=128 * a)
+        sca("tb", "idn", 128, y, a=128 * a)
+    for nm, x, y in (("ca", -512.0, None), ("cs", -32.0, None), ("ck2", 0.5, None), ("cb1", 1.5, 81.0)):
+        cst(nm, "cz", 1, x, y)
+    ts(col("cub"), col("cz"), 8.0, -(0.5 - 2.0 ** -12), OP.is_ge, OP.mult, 1, rd=["cz"], wr=["cub"])
+    cst("ct", "thb", 1, -1.0, 2048.0)
+    cst("tdg", "idn", 128, col("ct"), rd=["ct"])
+    fill("rsc1", M("rsc"), 1.0, 64)
+    fill("rsc", M("rsc", 15, 8, 16), 0.0, 8, wr=["rsc", "rsc1"])
+    for c in range(NCH):
+        fill("d0a", M("d0a", 6 * c * n, 3 * n), 0.0, 3 * n // 2, wr=[("d0a", c)])
+    fill("d0b", M("d0b", 0, C, 3), 0.0, C // 2, wr=[("d0b", c) for c in range(NCH)])
+    ts(M("d1", 2, C, 3), M("m64", 0, C), 0.0, None, OP.mult, None, C // 2, rd=["m64"], wr=[("d1", c) for c in range(NCH)], name="d1")
+    cst("s1", "idn", 128, col("cb1"), rd=["cb1"])
+    cst("lowh", "low", 128, 0.5)
+    tt(M("m1h"), M("s1"), M("lowh"), OP.add, 256, rd=["s1", "lowh"], wr=["m1h"])
+    cst("uph", "upp", 128, 0.5)
+    fill("one32", M("one32"), 1.0, 128)
+    ts(M("rst", 0, 512), M("m64", 0, 512), -8.0, None, OP.mult, None, 256, rd=["m64"], wr=["rst1"])
+    ts(M("rst", 0, 64, 8), M("m64", 0, 64), -1.0, None, OP.mult, None, 64, rd=["m64"], wr=["rst", "rst1"])
+    cst("j2", "j1", 128, -1.0, -1.0)
+    tt(M("j3"), M("j1"), M("j2"), OP.mult, 256, rd=["j1", "j2"], wr=["j3"])
+    tt(M("oth"), M("j3"), M("tmpb"), OP.mult, 256, rd=["j3", "tmpb"], wr=["oth"])
+    for j in range(2):
+        b = 4 + 2 + j
+        ms = []
+        for k in range(4):
+            ms += group(PS(b, 128 * k, 128), [(M("idn"), M("bo", 512 * j + 128 * k)), (M("idn"), M("oth"))], 128)
+        pe(ms, rd=["idn", "oth", "bo"] + [("bo", 128 * x) for x in range(1, 4 * j + 4)], wr=[("bap", j)], bank=[b], name="bap")
+        cp(M("ba", 512 * j, 512), PS(b, 0, 512), 512, rd=[("bap", j)], wr=[("ba", j)], bank=[b], name="ba")
+    act(M("s4"), M("s3"), AF.Abs, 128, rd=["s3"], wr=["s4"])
+    ts(M("s5"), M("s4"), col("cj"), None, OP.is_equal, None, 64, rd=["s4", "cj"], wr=["s5"])
+    ts(M("s6"), M("s3"), -2048.0, 1.0, OP.mult, OP.max, 64, rd=["s3"], wr=["s6"])
+    ts(M("s4"), M("s6"), 2048.0, None, OP.min, None, 64, rd=["s6"], wr=["s4"])
+    tt(M("s6"), M("s4"), M("s5"), OP.mult, 256, rd=["s4", "s5"], wr=["s6"])
+    tt(M("wn"), M("s6"), M("tmpb"), OP.mult, 256, rd=["s6", "tmpb"], wr=["wn"])
 
     for e_ in range(LE):
         for c in range(NCH):
             CUR["lc"] = (e_, c)
-            chunk(add, ts, vcost, gcost, pcost, e_, c, BP, wrprep, cy)
+            chunk(add, e_, c)
     return ops
 
 
-def count(add, vcost, pcost, e_):
-    def ff2(g, T, e):
-        ps = T["ps%d" % FB]
-        for c in range(NCH):
-            r = e.matmul(ps[:, UF + 1:UF + 2], T.one[:, 0:128], T.fs[:, e_ * NCH + c:e_ * NCH + c + 1], c == 0, c == NCH - 1)
-        return r
-    add("P", pcost(*[64] * NCH), ff2, rd=["one"] + [("fs", e_, c) for c in range(NCH)], wr=[("f2", e_)], bank=[FB], name="F2")
-    add("V", vcost(1), lambda g, T, e: e.tensor_copy(T.fi[:, e_:e_ + 1], T["ps%d" % FB][:, UF + 1:UF + 2]), rd=[("f2", e_)], wr=[("fi", e_)], bank=[FB], name="fi")
-    add("V", vcost(1), lambda g, T, e: e.tensor_scalar(T.fm[:, e_:e_ + 1], T.fi[:, e_:e_ + 1], 31, None, OP.bitwise_and), rd=[("fi", e_)], wr=[("fm", e_)], name="fm")
-    add("V", vcost(1), lambda g, T, e: e.tensor_scalar(T.tac[:, e_ + 1:e_ + 2], T.fm[:, e_:e_ + 1], 16.0, T.tcol[:, 0:1], OP.mult, OP.add),
-        rd=[("fm", e_), "tcol"], wr=[("tac", e_ + 1)], name="ta")
-
-
-def chunk(add, ts, vcost, gcost, pcost, e_, c, BP, wrprep, cy):
+def chunk(add, e_, c):
+    vec, ts, tt, cp, scan, act, pe, group = tools(add)
     i0 = c * n
     pr = e_ % 2
     o = pr * C + i0
@@ -226,159 +293,167 @@ def chunk(add, ts, vcost, gcost, pcost, e_, c, BP, wrprep, cy):
     last = e_ == LE - 1
     t = lambda nm, *x: (nm, pr, c) + x
     L, Z = ("lst", e_, c), ("zb", e_, c)
+    IND = lambda win, a, w, off, b, k: (lambda T: T[win][:, a:a + w].indirect(T[off][:, b:b + k]))
+    blocks = [(s, sum(XB[:s]), w) for s, w in enumerate(XB)]
+    xblocks = [(s, sum(XG[:s]), w) for s, w in enumerate(XG)]
+    XX = [t("xx", s) for s, a, w in xblocks]
+    G0, G1 = ("grp", R0), ("grp", R1)
 
-    def mm(out, lhs, rhs, start, stop):
-        return lambda T, e: e.matmul(out(T), lhs(T), rhs(T), start, stop)
+    pe([(PS(R0, 0, nq), M("bw", 15 - m), M("zb", lz + m, nq, 16), m == 0, m == 15, nq) for m in range(16)],
+       rd=["bw", Z], wr=[t("ul")], bank=[R0], acc=G0, name="UL")
+    cp(M("ci", ot, nq), PS(R0, 0, nq), nq, rd=[t("ul")], wr=[t("ci")], bank=[R0], name="ci")
+    ts(M("v5", ot, nq), M("ci", ot, nq), 31, None, OP.bitwise_and, None, nq, rd=[t("ci")], wr=[t("v5")], name="v5")
+    tt(M("vv", ot, nq), M("v5", ot, nq), M("v5", ot, nq), OP.mult, nq, rd=[t("v5")], wr=[t("vv")], name="vv")
+    ts(M("bi", ot, nq), M("vv", ot, nq), 5, 1, OP.arith_shift_right, OP.bitwise_and, nq, rd=[t("vv")], wr=[t("bi")], name="bi")
+    tt(M("cc", ot, nq), M("bi", ot, nq), M("io2", 0, nq), OP.add, nq, rd=[t("bi"), "io2"], wr=[t("cc")], name="cc")
+    cp(M("cl", o, nq), M("cc", ot, nq), nq, rd=[t("cc")], wr=[t("cl")], name="cl")
+    u37 = [(M("lwa"), M("zb", lz, n)), (M("lwb"), M("zb", lz, n))]
+    if UMOD:
+        pe(group(PS(R1, 128, n), [(M("lw"), M("zb", lz, n))], n), rd=["lw", Z], wr=[t("u0")], bank=[R1], acc=G1, name="U0")
+        act(M("uh", o, n), PS(R1, 128, n), AF.Copy, n, bias=128.0, scale=1.0 / 4096, rd=[t("u0")], wr=[t("uh")], bank=[R1], name="uh")
+        u37 = [(M("one"), M("icq")), (M("iq"), M("uh", o, n))] + u37
+    pe(group(PS(R0, 128, n), u37, n), rd=["lwa", "lwb", Z] + (["one", "icq", "iq", t("uh")] if UMOD else []), wr=[t("u37")], bank=[R0], acc=G0, name="U37")
 
-    def PS(b, a, w):
-        return lambda T: T["ps%d" % b][:, a:a + w]
-
-    def M(nm, a=0, w=128):
-        return lambda T: T[nm][:, a:a + w]
-
-    def Sx(nm, a, b, st):
-        return lambda T: T[nm][:, a:b:st]
-
-    def pe(mms, cols, **kw):
-        def f(g, T, e):
-            for m in mms:
-                r = m(T, e)
-            return r
-        add("P", pcost(*cols), f, **kw)
-
-    def group(out, pairs):
-        return [mm(out, l, r, i == 0, i == len(pairs) - 1) for i, (l, r) in enumerate(pairs)]
-
-    def act(out, src, func, m, bias=None, **kw):
-        def f(g, T, e):
-            if bias is None:
-                return e.activation(out(T), src(T), func)
-            return e.activation(out(T), src(T), func, bias=bias(T) if not isinstance(bias, float) else bias)
-        add("S", m * cy, f, **kw)
-
-    def vec(f, m, cyc=1.0, cost=None, **kw):
-        add("V", vcost(m, cyc) if cost is None else cost, lambda g, T, e: f(T, e), **kw)
-
-    pe(group(PS(R0, 0, nq), [(M("bw", 15 - m), Sx("zb", lz + m, lz + n, 16)) for m in range(16)]), [64] * 16, rd=["bw", Z], wr=[t("ul")], bank=[R0], name="UL")
-    vec(lambda T, e: e.tensor_copy(T.ci[:, ot:ot + nq], T["ps%d" % R0][:, 0:nq]), nq, rd=[t("ul")], wr=[t("ci")], bank=[R0], name="ci")
-    vec(lambda T, e: e.tensor_scalar(T.v5[:, ot:ot + nq], T.ci[:, ot:ot + nq], 31, None, OP.bitwise_and), nq, rd=[t("ci")], wr=[t("v5")], name="v5")
-    vec(lambda T, e: e.tensor_tensor(T.vv[:, ot:ot + nq], T.v5[:, ot:ot + nq], T.v5[:, ot:ot + nq], OP.mult), nq, 2, rd=[t("v5")], wr=[t("vv")], name="vv")
-    vec(lambda T, e: e.tensor_scalar(T.bi[:, ot:ot + nq], T.vv[:, ot:ot + nq], 5, 1, OP.arith_shift_right, OP.bitwise_and), nq, rd=[t("vv")], wr=[t("bi")], name="bi")
-    vec(lambda T, e: e.tensor_tensor(T.cc[:, ot:ot + nq], T.bi[:, ot:ot + nq], T.io2[:, 0:nq], OP.add), nq, 2, rd=[t("bi"), "io2"], wr=[t("cc")], name="cc")
-    oc = (pr * NCH + c) * n
-    vec(lambda T, e: e.tensor_copy(T.cl[:, oc:oc + nq], T.cc[:, ot:ot + nq]), nq, rd=[t("cc")], wr=[t("cl")], name="cl")
-    pe(group(PS(R0, 128, n), [(M("lwa"), M("zb", lz, n)), (M("lwb"), M("zb", lz, n))]), [n] * 2, rd=["lwa", "lwb", Z], wr=[t("u37")], bank=[R0], name="U37")
-
-    vec(lambda T, e: e.tensor_copy(T.k32[:, o:o + n], T.lst[:, lz:lz + n]), n, rd=[L], wr=[t("k32")], name="k32")
-    for s in range(NS_):
-        a = of + s * SB * 16
-        add("S", gcost(SB * 16), lambda g, T, e, a=a, s=s: e.activation(T.xx[:, a:a + SB * 16], T.gearb[:, 0:PAD + VX].indirect(T.lst[:, lz + s * SB:lz + s * SB + SB]), AF.Copy),
-            rd=["gearb", "gpad", L], wr=[t("xx", s)], name="x")
-    vec(lambda T, e: e.tensor_tensor(T.pp[:, o:o + n], T.rtb[:, 2 * i0:2 * i0 + 2 * n].indirect(T.cl[:, oc:oc + nq]), T.k32[:, o:o + n], OP.mult), n, cost=gcost(n),
-        rd=["rtb", t("cl"), t("k32")], wr=[t("pp")], name="P")
-    vec(lambda T, e: e.tensor_scalar(T.qq[:, o:o + n], T.pp[:, o:o + n], 5, None, OP.arith_shift_right), n, rd=[t("pp")], wr=[t("qq")], name="Q")
-    vec(lambda T, e: e.tensor_tensor(T.tt[:, o:o + n], T.qq[:, o:o + n], T["ps%d" % R0][:, 128:128 + n], OP.add), n, rd=[t("qq"), t("u37")], wr=[t("tt")], bank=[R0], name="T")
-    vec(lambda T, e: e.tensor_scalar(T.t2[:, o:o + n], T.tt[:, o:o + n], 4095, None, OP.bitwise_and), n, rd=[t("tt")], wr=[t("t2")], name="T2")
-    vec(lambda T, e: e.tensor_copy(T.sl[:, o:o + n], T.t2[:, o:o + n]), n, rd=[t("t2")], wr=[t("sl")], name="SL")
+    ts(M("k32", o, n), M("lst", lz, n), 32.0, None, OP.add, None, n, rd=[L], wr=[t("k32")], name="k32")
+    for s, a, w in xblocks:
+        act(M("xx", of + a * 16, w * 16), IND("gearb", 0, VX, "lst", lz + a, w), AF.Copy, w * 16, kind="g", rd=["gearb", L], wr=[t("xx", s)], name="x")
+    tt(M("pp", o, n), IND("rtb", 2 * i0, 2 * n, "cl", o, nq), M("k32", o, n), OP.mult, n, kind="g", rd=["rtb", t("cl"), t("k32")], wr=[t("pp")], name="P")
+    if UMOD:
+        tt(M("tt", o, n), M("pp", o, n), PS(R0, 128, n), OP.add, n, rd=[t("pp"), t("u37")], wr=[t("tt")], bank=[R0], name="T")
+        ts(M("t2", o, n), M("tt", o, n), 5, 4095, OP.arith_shift_right, OP.bitwise_and, n, rd=[t("tt")], wr=[t("t2")], name="T2")
+    else:
+        ts(M("qq", o, n), M("pp", o, n), 5, None, OP.arith_shift_right, None, n, rd=[t("pp")], wr=[t("qq")], name="Q")
+        tt(M("tt", o, n), M("qq", o, n), PS(R0, 128, n), OP.add, n, rd=[t("qq"), t("u37")], wr=[t("tt")], bank=[R0], name="T")
+        ts(M("t2", o, n), M("tt", o, n), 4095, None, OP.bitwise_and, None, n, rd=[t("tt")], wr=[t("t2")], name="T2")
+    cp(M("sl", o, n), M("t2", o, n), n, rd=[t("t2")], wr=[t("sl")], name="SL")
 
     for j in range(NB):
         b = (X0, X1)[j % 2]
-        ms, cols = [], []
+        ms = []
         for kk in range(KB):
             k = j * KB + kk
-            ms += group(PS(b, kk * n, n), [(M("idn"), Sx("xx", of + k, of + 16 * n, 16)), (M("idm"), M("zb", lz, n))])
-            cols += [n, n]
-        pe(ms, cols, rd=["idn", "idm", Z] + [t("xx", s) for s in range(NS_)], wr=[t("xz", j)], bank=[b], name="xz")
+            ms += group(PS(b, kk * n, n), [(M("idn"), M("xx", of + k, n, 16)), (M("idm"), M("zb", lz, n))], n)
+        pe(ms, rd=["idn", "idm", Z] + XX, wr=[t("xz", j)], bank=[b], acc=("grp", b), name="xz")
         for h in range(KB // 2):
             k = j * KB + 2 * h
-            bias = 0.5 - 16 * ((15 - k) // 2)
-            add("S", 2 * n * cy, lambda g, T, e, b=b, h=h, k=k, v=k // 2: e.activation(T.sg[:, of + k * n:of + k * n + 2 * n], T["ps%d" % b][:, 2 * h * n:2 * h * n + 2 * n],
-                AF.Sign, bias=T.mcol[:, v:v + 1] if False else 0.5 - 16 * ((15 - k) // 2)), rd=[t("xz", j)], wr=[t("sg", k // 2)], bank=[b], name="sg")
-        pe([mm(PS(R1, 0, n), M("bh", 15 - k), M("sg", of + k * n, n), k == 0, False) for k in range(j * KB, j * KB + KB)], [n] * KB,
-           rd=["bh"] + [t("sg", v) for v in range(j * KB // 2, j * KB // 2 + KB // 2)], wr=[t("cn", j)], bank=[R1], acc=("cn", e_, c), name="cnt")
+            act(M("sg", of + k * n, 2 * n), PS(b, 2 * h * n, 2 * n), AF.Sign, 2 * n, bias=0.5 - 16 * ((15 - k) // 2), rd=[t("xz", j)], wr=[t("sg", k // 2)],
+                bank=[b], name="sg")
+        ms = [(PS(R1, 0, 128), M("one"), M("im16"), True, False, 128)] if j == 0 else []
+        ms += [(PS(R1, k, 8, 16), M("sg", of + k * n, n), M("tmpb", 0, 8, 16), False, False, 8) for k in range(j * KB, j * KB + KB)]
+        pe(ms, rd=["one", "im16", "tmpb"] + [t("sg", v) for v in range(j * KB // 2, j * KB // 2 + KB // 2)], wr=[t("cn", j)], bank=[R1], acc=G1, name="cnt")
 
-    for s in range(NS_):
-        a = of + s * SB * 16
-        w = SB * 16
-        vec(lambda T, e, a=a, w=w, s=s: e.tensor_tensor(T.dd[:, a:a + w], T.siteb[:, 0:VY].indirect(T.sl[:, o + s * SB:o + s * SB + SB]), T.xx[:, a:a + w], OP.subtract), w, cost=gcost(w),
-            rd=["siteb", t("sl"), t("xx", s)], wr=[t("dd", s)], name="y")
-        ab = s in ABS_S
-        if ab:
+    ms = [(PS(R0, 256, 128), M("one"), M("tdg"), True, False, 128)]
+    rv = [b for b in blocks if (c, b[0]) in RELU_V]
+    for s, a, w in blocks:
+        a, w, a0, w0 = of + a * 16, w * 16, a, w
+        tt(M("dd", a, w), IND("siteb", 0, VY, "sl", o + a0, w0), M("xx", a, w), OP.subtract, w, kind="g", rd=["siteb", t("sl")] + [t("xx", x) for x, xa, xw in xblocks if xa < a0 + w0 and xa + xw > a0], wr=[t("dd", s)], name="y")
+        if (c, s) in RELU_V:
+            ts(M("da", a, w), M("dd", a, w), 0.0, 2.0, OP.max, OP.mult, w // 2, rd=[t("dd", s)], wr=[t("da", s)], name="relu")
+        else:
             act(M("da", a, w), M("dd", a, w), AF.Abs, w, rd=[t("dd", s)], wr=[t("da", s)], name="abs")
-            pairs = [(M("b1", 15 - k), Sx("da", a + k, a + w, 16)) for k in range(16)]
-        else:
-            vec(lambda T, e, a=a, w=w: e.tensor_scalar(T.da[:, a:a + w], T.dd[:, a:a + w], 0.0, None, OP.max), w, 0.5, rd=[t("dd", s)], wr=[t("da", s)], name="relu")
-            pairs = [(M("bn", 15 - k), Sx("dd", a + k, a + w, 16)) for k in range(16)] + [(M("b2", 15 - k), Sx("da", a + k, a + w, 16)) for k in range(16)]
-        if ab:
-            pe(group(PS(R0, 256 + s * SB, SB), pairs), [SB] * len(pairs), rd=["b1", t("da", s)], wr=[t("D", s)], bank=[R0], name="D")
-        else:
-            pe(group(PS(R0, 256 + s * SB, SB), pairs), [SB] * len(pairs), rd=["b2", "bn", t("dd", s), t("da", s)], wr=[t("D", s)], bank=[R0], name="D")
-    vec(lambda T, e: e.tensor_scalar(T.pm[:, o:o + n], T["ps%d" % R0][:, 256:256 + n], T.tac[:, e_:e_ + 1], -1.0, OP.is_lt, OP.add), n,
-        rd=[t("D", s) for s in range(NS_)] + [("tac", e_)], wr=[t("pm")], bank=[R0], name="p")
-    pe([mm(PS(R1, 0, n), M("i16"), M("pm", o, n), False, True)], [n], rd=["i16", t("pm")], wr=[t("cn")], bank=[R1], acc=("cn", e_, c), name="cnp")
-    act(M("hd", o, n), PS(R1, 0, n), AF.Relu, n, rd=[t("cn")], wr=[t("hd")], bank=[R1], name="hold")
-    pe(group(PS(R1, 128, n), [(M("i20"), M("pm", o, n)), (M("tri4"), M("hd", o, n))]), [n] * 2, rd=["tri4", "i20", t("hd"), t("pm")], wr=[t("H")], bank=[R1], name="H")
-    vec(lambda T, e: e.tensor_scalar(T.ff[:, o:o + n], T["ps%d" % R1][:, 128:128 + n], 0.0, None, OP.is_equal), n, rd=[t("H")], wr=[t("ff")], bank=[R1], name="f")
-    vec(lambda T, e: e.tensor_tensor(T.mk[:, o:o + n], T.k32[:, o:o + n], T["ps%d" % R1][:, 128:128 + n], OP.min), n, rd=[t("H"), t("k32")], wr=[t("mk")], bank=[R1], name="mk")
-    vec(lambda T, e: e.tensor_copy(T.hl[:, o:o + n], T.mk[:, o:o + n]), n, rd=[t("mk")], wr=[t("hl")], name="hl")
+    if rv:
+        p0, pw = rv[0][1], sum(b[2] for b in rv)
+        ms += [(lambda T, k=k: T["ps%d" % R0][p0:p0 + pw, 256 + k:256 + 128:16], M("dd", of + 16 * p0 + k, pw, 16), M("blkm", 0, 8, 16), False, False, 8) for k in range(16)]
+    pe(ms, rd=["one", "tdg", "blkm"] + [t("dd", b[0]) for b in rv], wr=[t("D0")], bank=[R0], acc=G0, name="D0")
+    pe([(PS(R0, 256 + k, 8, 16), M("da", of + k, n, 16), M("tmpb", 0, 8, 16), False, k == 15, 8) for k in range(16)],
+       rd=["tmpb"] + [t("da", s) for s, a, w in blocks], wr=[t("D")], bank=[R0], acc=G0, name="D")
+    act(M("pm", o, n), PS(R0, 256, n), AF.Sign, n, bias=2047.5 if e_ == 0 else M("tac", e_, 1), scale=-1.0, rd=[t("D")] + ([("tac", e_)] if e_ else []), wr=[t("pm")],
+        bank=[R0], name="p")
+    pe([(PS(R1, 0, 128), M("i16"), M("pm", o, n), False, True, n)], rd=["i16", t("pm")], wr=[t("cn")], bank=[R1], acc=G1, name="cnp")
+    pe([(PS(R0, 0, 2 * n), M("pm", o, n), M("ta", 0, 256), True, False, 2 * n)], rd=["ta", ("ta", 128), t("pm")], wr=[t("N0")], bank=[R0], acc=G0, name="N0")
+    scan(REV("sv", o, n), REV("rsc", 0, n), REV("ps%d" % R1, 0, n), 0.0, OP.mult, OP.max, n, rd=["rsc", t("cn")], wr=[t("sv")], bank=[R1], name="stop")
+    pe([(PS(R0, 0, 2 * n), M("sv", o, n), M("tb", 0, 256), False, True, 2 * n)], rd=["tb", ("tb", 128), t("sv")], wr=[t("N")], bank=[R0], acc=G0, name="N")
+    DA, DB, D1 = ("d0a", c), ("d0b", c), ("d1", c)
+    HS = lambda a=0, w=n: M("d0a", 6 * i0 + 3 * n + 1 + 3 * a, w, 3)
+    NF = M("d0a", 6 * i0 + 1, n, 3)
+    act(M("d0a", 6 * i0 + 1, 2 * n, 3), PS(R0, 0, 2 * n), AF.Sign, 2 * n, bias=8.0, rd=[t("N")], wr=[DA], bank=[R0], name="nfh")
+    act(M("d0b", 3 * i0 + 1, n, 3), PS(R0, 0, n), AF.Relu, n, bias=-7.0, scale=-1.0, acc_out=None if last else M("fs", e_ * NCH + c, 1), rd=[t("N")],
+        wr=[DB, ("fs", e_, c)], bank=[R0], name="f")
+    pe(group(PS(R1, 128, n), [(M("m1f"), NF), (M("m1h"), HS())], n) + group(PS(R1, 128 + n, n), [(M("m2f"), NF), (M("i32"), HS())], n),
+       rd=["m1f", "m1h", "m2f", "i32", DA], wr=[t("E")], bank=[R1], acc=G1, name="E")
+    act(M("rr", 2 * o, 2 * n), PS(R1, 128, 2 * n), AF.Relu, 2 * n, bias=-81.0, rd=[t("E")], wr=[t("rr")], bank=[R1], name="R")
+    pos = [(M("uph"), HS()), (M("idn"), M("rr", 2 * o, n)), (M("idn"), M("rr", 2 * o + n, n))]
+    PV = R0 if POS2 else R1
+    if POS2:
+        pe(group(PS(R0, 384, n), pos, n), rd=["uph", "idn", DA, t("rr")], wr=[t("pv")], bank=[R0], acc=G0, name="POSv")
+    pe(group(PS(R1, 384, n), pos, n), rd=["uph", "idn", DA, t("rr")], wr=[t("po")], bank=[R1], acc=G1, name="POS")
+    ts(M("d0b", 3 * i0 + 2, n, 3), PS(PV, 384, n), col("ck2"), 2.0 ** -11, OP.is_ge, OP.max, n, rd=[t("pv" if POS2 else "po"), "ck2"], wr=[DB], bank=[PV], name="mult")
+    act(M("aa", o, n), PS(R1, 384, n), AF.Abs, n, bias=col("ca"), scale=1024.0, rd=[t("po"), "ca"], wr=[t("aa")], bank=[R1], name="a")
+    act(M("ss", o, n), PS(R1, 384, n), AF.Square, n, bias=col("cs"), scale=64.0, rd=[t("po"), "cs"], wr=[t("ss")], bank=[R1], name="s")
     if e_ == 0:
-        wrprep(c)
-    vec(lambda T, e: e.tensor_scalar(T.k16[:, o:o + n], T.lst[:, lz:lz + n], -float(PAD), None, OP.add), n, 0.5, rd=[L], wr=[t("k16")], name="k16")
-    add("S", gcost(n), lambda g, T, e: e.activation(T.wg[:, o:o + n], T.wrb[:, 2 * i0:2 * i0 + 2 * n].indirect(T.cl[:, oc:oc + nq]), AF.Copy), rd=[("wrb", c), t("cl")], wr=[t("wg")],
-        name="wg")
-    vec(lambda T, e: e.tensor_tensor(T.dk[:, o:o + n], T.wrb[:, 2 * i0:2 * i0 + 2 * n].indirect(T.cl[:, oc:oc + nq]), T.k32[:, o:o + n], OP.subtract), n, cost=gcost(n),
-        rd=[("wrb", c), t("cl"), t("k32")], wr=[t("dk")], name="dk")
-    vec(lambda T, e: e.tensor_tensor(T.fd[:, o:o + n], T.dk[:, o:o + n], T.ff[:, o:o + n], OP.mult), n, 2, rd=[t("dk"), t("ff")], wr=[t("fd")], name="fd")
-    vec(lambda T, e: e.tensor_tensor(T.va[:, o:o + n], T.k16[:, o:o + n], T.fd[:, o:o + n], OP.add), n, 2, rd=[t("k16"), t("fd")], wr=[t("va")], name="va")
-    pe(group(PS(R0, 0, n), [(M("low"), M("pm", o, n)), (M("i64"), M("ff", o, n))]) + group(PS(R0, n, n), [(M("im64"), M("pm", o, n)), (M("upp"), M("ff", o, n))]),
-       [n] * 4, rd=["low", "i64", "im64", "upp", t("pm"), t("ff")], wr=[t("E")], bank=[R0], name="E")
+        cp(M("wrb", 2 * i0, 2 * n), M("wri", 2 * i0, 2 * n), 2 * n, rd=["wri"], wr=[("wrb", c)], name="wrb")
+    cp(M("d1", 3 * i0 + 1, n, 3), M("lst", lz, n), n // 2, rd=[L], wr=[D1], name="k16")
+    tt(M("d1", 3 * i0, n, 3), IND("wrb", 2 * i0, 2 * n, "cl", o, nq), M("d1", 3 * i0 + 1, n, 3), OP.subtract, n, kind="g", rd=[("wrb", c), t("cl")], wr=[D1], name="dk")
+    scan(M("ob", 3 * o, 3 * n), M("d0b", 3 * i0, 3 * n), M("d1", 3 * i0, 3 * n), 0.0, OP.mult, OP.subtract, 3 * n // 2, rd=[DB, D1], wr=[t("ob")], name="v")
+
+    def held(bb, q):
+        b = ((X0, X1)[q] + 4 * bb * XMX) % 8
+        pe([(PS(b, kk, 64, 8), M("ih"), M("xx", of + 1024 * bb + 8 * q + kk, 64, 16), kk == 0, False, 64) for kk in range(8)],
+           rd=["ih"] + XX, wr=[t("xp", bb, q)], bank=[b], acc=("grp", b), name="xp")
+        pe([(PS(b, kk, 64, 8), M("bkh", 128 * (8 * q + kk)), HS(64 * bb, 64), False, kk == 7, 64) for kk in range(8)],
+           rd=[("bkh", 1024) if q else "bkh", DA], wr=[t("xm", bb, q)], bank=[b], acc=("grp", b), name="xm")
+        a = of + 512 * bb
+        if not ESPLIT:
+            scan(M("xs", a + 8 * n * q, 512), M("rst", 0, 512), PS(b, 0, 512), 64.0, OP.min, OP.max, 512, rd=["rst", t("xm", bb, q)], wr=[t("xs", bb, q)],
+                 bank=[b], name="scan")
+        elif q == 0:
+            act(M("xs", a + 8 * n, 512), PS(b, 0, 512), AF.Copy, 512, rd=[t("xm", bb, q)], wr=[t("xs", bb, 1)], bank=[b], name="ev")
+        else:
+            tt(M("xs", a + 8 * n, 512), M("xs", a + 8 * n, 512), PS(b, 0, 512), OP.max, 512, rd=[t("xm", bb, q)], wr=[t("xs", bb, 1)], bank=[b], name="pair")
+            scan(M("xs", a, 512), M("rst", 0, 512), M("xs", a + 8 * n, 512), 64.0, OP.min, OP.max, 256, rd=["rst", t("xs", bb, 1)], wr=[t("xs", bb, 0)], name="scan")
+
+    def pick(j):
+        b = ((X0, X1)[j % 2] + 4 * CDX) % 8
+        k0, PW = sum(x[1] for x in PICK[:j]), PICK[j][1]
+        ms = []
+        for kk in range(PW):
+            k = k0 + kk
+            ms += group(PS(b, kk * n, n), [(M("ba", 128 * k), M("aa", o, n)), (M("bs", 128 * k), M("ss", o, n)), (M("bs", 128 * k), M("ob", 3 * o + 2, n, 3))], n)
+        pe(ms, rd=[("ba", 0), ("ba", 1), "bs", t("aa"), t("ss"), t("ob")], wr=[t("cd", j)], bank=[b], acc=("grp", b), name="cd")
+        a, w = 8 * o + k0 * n, PW * n
+        if PICK[j][0] == "S":
+            act(M("kl", a, w), PS(b, 0, w), AF.Relu, w, scale=1.0 / 64, rd=[t("cd", j)], wr=[t("kl", j)], bank=[b], name="pick")
+        else:
+            ts(M("kl", a, w), PS(b, 0, w), 0.0, 1.0 / 64, OP.max, OP.mult, w, rd=[t("cd", j)], wr=[t("kl", j)], bank=[b], name="pick")
+        pe([(PS(R1, 0, n), M("wn"), M("kl", 8 * o + k * n, n), k == 0, k == 7, n) for k in range(k0, k0 + PW)], rd=["wn", t("kl", j)],
+           wr=[t("nm") if j == len(PICK) - 1 else t("nm", j)], bank=[R1], acc=G1, name="NM")
+
+    for j in range(HELD1):
+        held(j // 2, j % 2)
+    if HELD1 < 4:
+        for j in range(len(PICK)):
+            pick(j)
+    for j in range(HELD1, 4):
+        held(j // 2, j % 2)
+    XS = [t("xs", bb, q) for bb in range(n // 64) for q in range(2)]
+    if not ESPLIT:
+        tt(M("mm", o, n), M("xs", of + 7, n, 8), M("xs", of + 8 * n + 7, n, 8), OP.max, 2 * n, rd=XS, wr=[t("mm")], name="mm")
+    pe(group(PS(R0, 256, n), [(M("idn"), M("zb", lz, n)), (M("im2"), M("xs", of + 7, n, 8) if ESPLIT else M("mm", o, n))], n), rd=["idn", "im2", Z, t("mm")] + XS, wr=[t("zn")], bank=[R0], acc=G0, name="ZN")
+    act(M("zsend", lz, n), PS(R0, 256, n), AF.Abs, n, bias=128.0, rd=[t("zn")], wr=[("zsend", e_, c)], bank=[R0], name="z'")
+    if not last and c == NCH - 1:
+        pe(group(PS(FB, 0, NCH), [(M("one32"), M("fs", e_ * NCH, NCH))], 256), rd=["one32"] + [("fs", e_, x) for x in range(NCH)],
+           wr=[("f2", e_)], bank=[FB], acc=G0, name="F2")
+        ts(M("fi", e_, 1), PS(FB, 0, 1), PS(FB, 1, 1), None, OP.add, None, 1, rd=[("f2", e_)], wr=[("fi", e_)], bank=[FB], name="fi")
+        ts(M("fm", e_, 1), M("fi", e_, 1), 31, None, OP.bitwise_and, None, 1, rd=[("fi", e_)], wr=[("fm", e_)], name="fm")
+        ts(M("tac", e_ + 1, 1), M("fm", e_, 1), 16.0, 2047.5, OP.mult, OP.add, 1, rd=[("fm", e_)], wr=[("tac", e_ + 1)], name="ta")
+    if HELD1 == 4:
+        for j in range(len(PICK)):
+            pick(j)
+    ts(M("ui", o, n), PS(R1, 0, n), col("cub"), None, OP.add, None, n, rd=[t("nm"), "cub"], wr=[t("ui")], bank=[R1], name="ui")
+    ts(M("uj", o, n), M("ui", o, n), 2047, None, OP.bitwise_and, None, n, rd=[t("ui")], wr=[t("uj")], name="uj")
+    scan(M("oa", 3 * o, 3 * n), M("d0a", 6 * i0, 3 * n), M("d1", 3 * i0, 3 * n), 0.0, OP.mult, OP.add, 3 * n // 2, rd=[DA, D1], wr=[t("oa")], name="w'")
+    cp(IND("wrb", 2 * i0, 2 * n, "cl", o, nq), M("oa", 3 * o + 1, n, 3), n, kind="s", rd=[t("cl"), t("oa")], wr=[("wrb", c)], name="scat")
     if not last:
-        pe([mm(lambda T: T["ps%d" % R0][0:n, UF:UF + 1], M("ff", o, n), M("one", 0, 1), True, True)], [64], rd=["one", t("ff")], wr=[t("fp")], bank=[R0], name="F1")
-        act(lambda T: T.fs[0:n, e_ * NCH + c:e_ * NCH + c + 1], lambda T: T["ps%d" % R0][0:n, UF:UF + 1], AF.Copy, 1, rd=[t("fp")], wr=[("fs", e_, c)], bank=[R0], name="fs")
-        if c == NCH - 1:
-            count(add, vcost, pcost, e_)
-    act(M("rr", 2 * o, 2 * n), PS(R0, 0, 2 * n), AF.Relu, 2 * n, bias=lambda T: T.c64[:, 0:1], rd=[t("E"), "c64"], wr=[t("rr")], bank=[R0], name="R")
-    pe(group(PS(R0, 256, n), [(M("upp"), M("pm", o, n)), (M("upm"), M("ff", o, n)), (M("idn"), M("rr", 2 * o, n)), (M("idn"), M("rr", 2 * o + n, n))]),
-       [n] * 4, rd=["upp", "upm", "idn", t("pm"), t("ff"), t("rr")], wr=[t("po0")], bank=[R0], name="POS")
-    act(M("po", o, n), PS(R0, 256, n), AF.Identity, n, bias=lambda T: T.c15[:, 0:1], rd=[t("po0"), "c15"], wr=[t("po")], bank=[R0], name="po")
-    for s in range(NS_):
-        a = of + s * SB * 16
-        w = SB * 16
-        add("S", gcost(w), lambda g, T, e, a=a, w=w, s=s: e.activation(T.xh[:, a:a + w], T.gearb[:, 0:PAD + VX].indirect(T.hl[:, o + s * SB:o + s * SB + SB]), AF.Copy),
-            rd=["gearb", "gpad", t("hl")], wr=[t("xh", s)], name="xh")
-        vec(lambda T, e, a=a, w=w: e.tensor_tensor_scan(T.xs[:, a:a + w], T.rst[:, 0:w], T.xh[:, a:a + w], 0.0, OP.mult, OP.max), w, 0.5, rd=["rst", t("xh", s)], wr=[t("xs", s)], name="scan")
-    pe(group(PS(R0, 384, n), [(M("idn"), M("zb", lz, n)), (M("idm"), Sx("xs", of + 15, of + 16 * n, 16))]), [n] * 2, rd=["idn", "idm", Z] + [t("xs", s) for s in range(NS_)],
-       wr=[t("zn")], bank=[R0], name="ZN")
-    zo = e_ * C + i0
-    act(M("zsend", zo, n), PS(R0, 384, n), AF.Abs, n, rd=[t("zn")], wr=[("zsend", e_, c)], bank=[R0], name="z'")
-    for j in range(NB):
-        b = (X0, X1)[j % 2]
-        ms, cols = [], []
-        for kk in range(KB):
-            k = j * KB + kk
-            ms += group(PS(b, kk * n, n), [(M("bp", 128 * k), M("po", o, n)), (M("bk", 128 * k), M("va", o, n))])
-            cols += [n, n]
-        pe(ms, cols, rd=BP + ["bk", t("po"), t("va")], wr=[t("cd", j)], bank=[b], name="cd")
-        a = of + j * 512
-        vec(lambda T, e, a=a, b=b: e.tensor_scalar(T.kl[:, a:a + 512], T["ps%d" % b][:, 0:512], 0.0, 2048.0, OP.max, OP.min), 512, rd=[t("cd", j)], wr=[t("kl", j)], bank=[b], name="clamp")
-        pe([mm(PS(R1, 256, n), M("idn"), M("kl", of + k * n, n), k == 0, k == 15) for k in range(j * KB, j * KB + KB)], [n] * KB, rd=["idn", t("kl", j)],
-           wr=[t("nm") if j == NB - 1 else t("nm", j)], bank=[R1], acc=("nm", e_, c), name="NM")
-    vec(lambda T, e: e.tensor_tensor(T.wrb[:, 2 * i0:2 * i0 + 2 * n].indirect(T.cl[:, oc:oc + nq]), T.wg[:, o:o + n], T.fd[:, o:o + n], OP.subtract), n, cost=0.05 + n * CFG["sc"] * cy,
-        rd=[t("cl"), t("wg"), t("fd")], wr=[("wrb", c)], name="scat")
-    if not last:
-        vec(lambda T, e: e.tensor_scalar(T.lsend[:, zo:zo + n], T["ps%d" % R1][:, 256:256 + n], T.cnm[:, 0:1], None, OP.add), n, rd=[t("nm"), "cnm"], wr=[("lsend", e_, c)],
-            bank=[R1], name="K'")
+        cp(M("lsend", lz, n), M("uj", o, n), n, rd=[t("uj")], wr=[("lsend", e_, c)], name="K'")
         for kind, src, dst in (("z", "zsend", "zb"), ("k", "lsend", "lst")):
-            add("G", 0.3, lambda g, T, e, src=src, dst=dst, kind=kind: (g, T[dst][:, zo + C:zo + C + n], T[src][:, zo:zo + n], "a%s%d_%d" % (kind, e_ + 1, c)),
-                rd=[(src, e_, c)], wr=[(dst, e_ + 1, c)], name="send" + kind, lat=CFG["net"], sem="a%s%d_%d" % (kind, e_ + 1, c), inc="net")
+            add("G", ("net", 0), lambda g, T, e, src=src, dst=dst: [(T[dst][:, lz + C:lz + C + n], T[src][:, lz:lz + n])],
+                rd=[(src, e_, c)], wr=[(dst, e_ + 1, c)], name="send" + kind, sem="a%s%d_%d" % (kind, e_ + 1, c), inc="net")
     else:
-        vec(lambda T, e: e.tensor_scalar(T.yks[:, i0:i0 + n], T["ps%d" % R1][:, 256:256 + n], T.cny[:, 0:1], None, OP.add), n, rd=[t("nm"), "cny"], wr=[("yks", c)],
-            bank=[R1], name="yk")
-        act(M("yws", 2 * i0, 2 * n), M("wrb", 2 * i0, 2 * n), AF.Copy, 2 * n, bias=-float(PAD), rd=[("wrb", c)], wr=[("yws", c)], name="yw")
-        for q, (dst, src, tok, a, b, sa) in enumerate((("yz", "zsend", ("zsend", e_, c), i0, i0 + n, zo), ("yw", "yws", ("yws", c), 2 * i0, 2 * i0 + 2 * n, 2 * i0),
-                                                 ("yk", "yks", ("yks", c), i0, i0 + n, i0))):
-            add("D", 0.0, lambda g, T, e, dst=dst, src=src, a=a, b=b, sa=sa: e.dma_start(T[dst][:, a:b], T[src][:, sa:sa + b - a]), rd=[tok], wr=[(dst, c)], name="store " + dst, lat=2.0,
-                sem="st%d" % (3 * c + q), inc=16)
+        cp(M("yks", i0, n), M("uj", o, n), n, rd=[t("uj")], wr=[("yks", c)], name="yk")
+        for q, (dst, src, tok, a, w, sa) in enumerate((("yz", "zsend", ("zsend", e_, c), i0, n, lz), ("yw", "wrb", ("wrb", c), 2 * i0, 2 * n, 2 * i0),
+                                                       ("yk", "yks", ("yks", c), i0, n, i0))):
+            add("D", ("dma", 2.0), lambda g, T, e, dst=dst, src=src, a=a, w=w, sa=sa: e.dma_start(T[dst][:, a:a + w], T[src][:, sa:sa + w]), rd=[tok], wr=[(dst, c)],
+                name="store " + dst, sem="st%d" % (3 * c + q), inc=16)
 
 
 def depend(ops):
@@ -409,41 +484,93 @@ def depend(ops):
         if op["acc"] is not None:
             if op["acc"] in last:
                 op["ord"].add(last[op["acc"]])
-                d.discard(last[op["acc"]])
             last[op["acc"]] = i
 
 
 def order(ops):
+    place, early, seen, key = {}, {}, {}, []
+    words = ROUND.split()
+    for p, w in enumerate(words):
+        place[w.strip("<>")] = p + len(words) * (w.count(">") - w.count("<"))
+    wait = []
+    for w in START.split():
+        if w[0] == "|":
+            nm, i = w[1:].split(":")
+            for j, x in enumerate(wait):
+                early[x] = place[nm] + len(words) * int(i) - 0.9 + 0.01 * j
+            wait = []
+        else:
+            wait.append(w)
+    for op in ops:
+        e, c = op["lc"]
+        k = seen.get((e, c, op["name"]), 0)
+        seen[(e, c, op["name"])] = k + 1
+        u = op["name"] + (str(k) if k else "")
+        u = u.replace("store ", "st_").replace("load ", "ld_").replace("aff ", "").replace("iota ", "").replace("('", "").replace("', ", "_").replace(")", "")
+        key.append(early[u] if e < 0 else place[u] + len(words) * (NCH * e + c))
+    succ = [[] for _ in ops]
+    left = []
+    for i, op in enumerate(ops):
+        left.append(len(op["dep"] | op["ord"]))
+        for j in op["dep"] | op["ord"]:
+            succ[j].append(i)
+    ready = [i for i in range(len(ops)) if left[i] == 0]
+    seq = []
+    while ready:
+        i = min(ready, key=lambda x: (key[x], x))
+        ready.remove(i)
+        seq.append(i)
+        for j in succ[i]:
+            left[j] -= 1
+            if left[j] == 0:
+                ready.append(j)
+    return seq, 0.0
+
+
+def order_greedy(ops):
     N_ = len(ops)
     succ = [[] for _ in range(N_)]
     for i, op in enumerate(ops):
         for j in op["dep"] | op["ord"]:
             succ[j].append(i)
+    wake = CFG["wake"]
     prio = [0.0] * N_
     for i in range(N_ - 1, -1, -1):
-        prio[i] = ops[i]["dur"] + ops[i]["lat"] + max([prio[j] + CFG["wake"] for j in succ[i]] or [0.0])
+        e, c = ops[i]["lc"]
+        if e >= 0:
+            prio[i] = ops[i]["dur"] + ops[i]["lat"] + max([prio[j] + wake for j in succ[i] if ops[j]["lc"][1] == c] or [0.0])
+    top = {}
     for i in range(N_):
-        prio[i] += BIAS.get((ops[i]["name"], ops[i]["lc"][1]), 0.0)
+        if ops[i]["name"] == "k32":
+            top[ops[i]["lc"]] = prio[i]
+    for i in range(N_ - 1, -1, -1):
+        e, c = ops[i]["lc"]
+        if e >= 0:
+            prio[i] += (LE - e - c / NCH) * CFG["T"] - top[(e, c)] + BIAS.get((ops[i]["name"], c), BIAS.get(ops[i]["name"], 0.0)) + BIAS.get((e, c), 0.0)
+        else:
+            prio[i] = ops[i]["dur"] + ops[i]["lat"] + max([prio[j] + wake for j in succ[i]] or [0.0])
     free, done, left = {}, [0.0] * N_, [len(op["dep"] | op["ord"]) for op in ops]
-    phys = {"E": "S"}
+    qu = [{"E": "S"}.get(op["e"], op["e"]) for op in ops]
     ready = {}
     rt = [0.0] * N_
     for i in range(N_):
         if left[i] == 0:
-            ready.setdefault(phys.get(ops[i]["e"], ops[i]["e"]), []).append(i)
+            ready.setdefault(qu[i], []).append(i)
     seq = []
     while len(seq) < N_:
         best = None
         for q, lst in ready.items():
             if not lst:
                 continue
-            f = free.get(q, 0.0)
-            m = min(max(f, rt[i]) for i in lst)
+            m = max(free.get(q, 0.0), min(rt[i] for i in lst))
             if best is None or m < best[0]:
                 best = (m, q)
         m, q = best
-        cand = [i for i in ready[q] if max(free.get(q, 0.0), rt[i]) <= m + 1e-9]
-        i = max(cand, key=lambda x: prio[x])
+        i = max((x for x in ready[q] if rt[x] <= m + 1e-9), key=lambda x: prio[x])
+        soon = [x for x in ready[q] if prio[x] > prio[i] + CFG["gap"] and rt[x] <= m + CFG["look"] * ops[i]["dur"]]
+        if soon:
+            i = min(soon, key=lambda x: rt[x])
+            m = max(m, rt[i])
         ready[q].remove(i)
         op = ops[i]
         end = m + op["dur"]
@@ -453,9 +580,9 @@ def order(ops):
         seq.append(i)
         for j in succ[i]:
             left[j] -= 1
-            rt[j] = max(rt[j], done[i] + CFG["wake"])
+            rt[j] = max(rt[j], done[i] + wake if i in ops[j]["dep"] else end)
             if left[j] == 0:
-                ready.setdefault(phys.get(ops[j]["e"], ops[j]["e"]), []).append(j)
+                ready.setdefault(qu[j], []).append(j)
     return seq, max(done)
 
 
@@ -513,9 +640,9 @@ def rank_program(g, core, T, topo):
         for s, v in waits:
             q.wait_ge(T.sem[s], neng_in if s[0] == "a" else v)
         if op["inc"] == "net":
-            _g, out, in_, rs = op["fn"](g, T, q)
-            g.remote_dma(out, in_, T.sem[rs], T.sem.sent, pid, rid, emask)
-            sent += len(eng)
+            for out, in_ in op["fn"](g, T, q):
+                g.remote_dma(out, in_, T.sem[op["sem"]], T.sem.sent, pid, rid, emask)
+                sent += len(eng)
         else:
             r = op["fn"](g, T, q)
             if op["sem"] is None:

from concourse.bass import DstId, RemoteDMATransfer
from concourse.mybir import dt, AluOpType as OP, AxisListType, ActivationFunctionType as AF

VX, VY, C, LE = 2048, 4096, 256, 5
NCH = 2
n = C // NCH
XG = (32, 32, 32, 32)
XB = (32, 32, 64)
nq = n // 16
KB = 512 // n
NB = 16 // KB
RELU_V = {(0, 2), (1, 2)}
HELD1 = 4
PICK = (("S", 3), ("S", 3), ("S", 2))
UMOD = True
ESPLIT = False
CDX = 0
XMX = 1
POS2 = False
ROUND = """
xp3 D0 D p wrb ta> scat> cnt2 cnt3 <U0 cnp <UL stop dk <ci <uh N0 N nfh xp1 xp xm <v5 sendk> <k32 <x1 <vv E R xm1 <bi <U37 f POS <cc xp2 scan scan1
xm3 <cl mult <x a s <P v <T <x2 scan3 xm2 <T2 cd pick <x3 scan2 cd1 pick1 cd2 pick2 <SL NM mm ZN z' st_yz st_yw> <y <y1 sendz <xz <sg <sg1 NM1 NM2
<xz1 ui <sg2 <sg3 uj K' <y2 <k16 <cnt <abs1 <relu F2 fi <abs <xz2 <sg4 w' yk st_yk <sg5 <xz3 <sg6 <sg7 <cnt1 fm
"""
START = """
one rsc1 m64 d0a_1 d0b_0 d0a_0 rst1 kf k15 ld_z0 ld_wt cz wcol |U0:0 rsc idn tmpa iq idm im16 i16 ta tb tmpb blkm ld_rk lst0 b1 bw k8 rst cb1 lw
ta_128 cj wa |ci:0 icq io1 io2 |uh:0 s1 wac |bi:0 wb |U37:0 ck2 |cl:0 lwa ld_gx lwb tb_128 ld_rt ld_sy ld_th |P:0 one32 lst01 |T:0 d1 |x2:0 im2 |x3:0
j1 s3 j2 s6 cub j3 |SL:0 ih i32 oth |y:0 s4 |y1:0 ct ld_wr |xz:0 tdg s5 |k16:0 low lowh s41 |sg5:0 upp |xz3:0 s61 |U0:1 m1h |cnp:0 m1f m2f bkh wn bkh1
own bo |stop:0 bo1 bo2 bo3 bo4 bap |N0:0 cs |v5:1 ca |k32:1 uph bo5 |E:0 bo6 bo7 bap1 |U37:1 ba |f:0 bs |scan1:0 ba1 |cl:1
"""
CFG = {"fix": {"V": 0.03, "S": 0.05, "P": 0.0, "G": 0.05, "D": 0.06, "E": 0.06}, "pe": 0.417e-3 * 1.15, "cy": 0.83e-3 * 1.15, "ga": 1.56,
       "sc": 3.8, "wake": 0.08, "net": 2.6, "T": 20.0, "gap": 1.0, "look": 0.4}
FB = 4 * ((NCH - 1) % 2)
CUR = {"lc": (0, 0)}
CACHE = {}
BIAS = {("nfh", 1): -6, ("scan", 0): 1.3, ("w'", 0): -18, ("y", 0): -1.4, ("Q", 1): -6, ("a", 0): 3, ("xm", 0): -1, ("k32", 1): -9, ("k16", 0): -11.4,
        ("Q", 0): 4.7, ("abs", 0): -2, ("stop", 0): -1, ("F2", 1): -14, ("cl", 0): -6, ("k16", 1): -4, ("cd", 0): 2, ("ZN", 0): 20, ("mm", 0): 8,
        ("wrb", 1): -11, ("dk", 0): -8, ("NM", 0): 2, ("D", 0): -4, ("yk", 0): -13, ("wrb", 0): 2, ("T", 1): 3, ("POS", 1): 5, ("E", 1): 4,
        ("scan", 1): 0.4, ("mult", 0): 2}

SCRATCH = {}
for _nm, _dt, _co in (
        ("gearb", "bfloat16", VX), ("siteb", "bfloat16", VY), ("rkb", "int32", C), ("rtb", "int32", 2 * C), ("wri", "int32", 2 * C),
        ("wrb", "float32", 2 * C), ("wtb", "bfloat16", 2), ("thb", "int32", 2), ("tac", "float32", 8),
        ("lst", "uint16", LE * C), ("lsend", "uint16", LE * C), ("zb", "bfloat16", LE * C), ("zsend", "bfloat16", LE * C),
        ("ci", "int32", 2 * NCH * nq), ("v5", "int32", 2 * NCH * nq), ("vv", "int32", 2 * NCH * nq), ("bi", "int32", 2 * NCH * nq),
        ("cc", "int32", 2 * NCH * nq), ("cl", "uint16", 2 * C),
        ("k32", "float32", 2 * C), ("pp", "int32", 2 * C), ("qq", "int32", 2 * C), ("tt", "int32", 2 * C),
        ("t2", "int32", 2 * C), ("sl", "uint16", 2 * C),
        ("xx", "bfloat16", 32 * C), ("dd", "bfloat16", 32 * C), ("da", "bfloat16", 32 * C), ("sg", "bfloat16", 32 * C),
        ("pm", "bfloat16", 2 * C), ("sv", "bfloat16", 2 * C), ("rr", "bfloat16", 4 * C), ("aa", "bfloat16", 2 * C), ("ss", "bfloat16", 2 * C),
        ("d0a", "bfloat16", 6 * C), ("d0b", "bfloat16", 3 * C), ("d1", "float16", 3 * C), ("oa", "float16", 6 * C), ("ob", "float16", 6 * C),
        ("xs", "float16", 32 * C), ("mm", "float16", 2 * C), ("kl", "float16", 16 * C), ("ui", "int32", 2 * C), ("uj", "int32", 2 * C),
        ("yks", "float32", C), ("fs", "float32", LE * NCH), ("fi", "int32", LE), ("fm", "int32", LE),
        ("one", "bfloat16", 144), ("one32", "float32", 128), ("m64", "bfloat16", 2048), ("b1", "bfloat16", 144),
        ("bw", "bfloat16", 144), ("tmpa", "bfloat16", 144), ("tmpb", "bfloat16", 144), ("blkm", "bfloat16", 128),
        ("idn", "bfloat16", 128), ("idm", "bfloat16", 128), ("i16", "bfloat16", 128), ("im16", "bfloat16", 128), ("i32", "bfloat16", 128),
        ("ih", "bfloat16", 128), ("im2", "bfloat16", 128), ("im32", "bfloat16", 128), ("lowh", "bfloat16", 128), ("lw", "bfloat16", 128),
        ("iq", "bfloat16", 128), ("icq", "bfloat16", 128), ("uh", "bfloat16", 2 * C),
        ("ta", "bfloat16", 256), ("tb", "bfloat16", 256), ("tdg", "float16", 128),
        ("low", "bfloat16", 128), ("upp", "bfloat16", 128), ("m1f", "bfloat16", 128), ("m1h", "bfloat16", 128), ("m2f", "bfloat16", 128),
        ("uph", "bfloat16", 128), ("s1", "bfloat16", 128), ("s2", "bfloat16", 128), ("s3", "bfloat16", 128), ("s4", "bfloat16", 128),
        ("s5", "bfloat16", 128), ("s6", "bfloat16", 128), ("j1", "bfloat16", 128), ("j2", "bfloat16", 128), ("j3", "bfloat16", 128),
        ("own", "bfloat16", 128), ("oth", "bfloat16", 128), ("wn", "bfloat16", 128),
        ("bkh", "bfloat16", 2048), ("bs", "bfloat16", 1024), ("bo", "bfloat16", 1024), ("ba", "float16", 1024),
        ("w37", "float32", 2), ("wa", "bfloat16", 2), ("wb", "float32", 2), ("wac", "float32", 2), ("wcol", "float32", 2),
        ("lwa", "bfloat16", 128), ("lwb", "bfloat16", 128),
        ("rst", "float16", 512), ("rsc", "bfloat16", 128), ("io1", "int32", nq), ("io2", "int32", nq), ("kf", "int32", 2), ("k15", "int32", 2),
        ("cz", "float32", 2), ("k8", "int32", 2),
        ("ct", "float32", 2), ("cr", "float32", 2), ("ca", "float32", 2), ("cs", "float32", 2), ("ck2", "float32", 2), ("cb1", "float32", 2),
        ("cub", "float32", 2), ("cj", "float32", 2)):
    SCRATCH[_nm] = ("sbuf", [128, _co], _dt)
for _b in range(8):
    SCRATCH["ps%d" % _b] = ("psum", [128, 512], "float32")

LOADS = ("gear", "site", "rk", "rt", "wr", "z", "wt", "th")
SEMAPHORES = ["sV", "sS", "sP", "sG", "sent"] + ["ld_" + x for x in LOADS] + ["st%d" % i for i in range(3 * NCH)]
SEMAPHORES += ["a%s%d_%d" % (k, e, c) for k in "kz" for e in range(1, LE) for c in range(NCH)]


def cost(op, cfg):
    kind, m = op["c"]
    cy = cfg["cy"]
    d = {"v": lambda: max(64, m) * cy, "g": lambda: 0.03 + m * cfg["ga"] * cy, "s": lambda: 0.03 + m * cfg["sc"] * cy,
         "p": lambda: sum(max(64, x) for x in m) * cfg["pe"], "G": lambda: 0.15 + 2 * m * cy, "net": lambda: 0.3, "dma": lambda: 0.0}[kind]()
    return d + cfg["fix"][op["e"]], cfg["net"] if kind == "net" else (m if kind == "dma" else 0.0)


def M(nm, a=0, w=128, st=1):
    if st == 1:
        return lambda T: T[nm][:, a:a + w]
    return lambda T: T[nm][:, a:a + st * (w - 1) + 1:st]


def REV(nm, a, w):
    return lambda T: T[nm][:, a + w - 1:(a - 1 if a else None):-1]


def PS(b, a, w, st=1):
    return M("ps%d" % b, a, w, st)


def col(nm):
    return M(nm, 0, 1)


def at(x, T):
    return x if isinstance(x, (int, float)) or x is None else x(T)


def tools(add):
    def vec(f, m, kind="v", **kw):
        add("V", (kind, m), lambda g, T, e: f(T, e), **kw)

    def ts(out, src, s1, s2, o1, o2, m, **kw):
        if o2 is None:
            vec(lambda T, e: e.tensor_scalar(out(T), src(T), at(s1, T), None, o1), m, **kw)
        else:
            vec(lambda T, e: e.tensor_scalar(out(T), src(T), at(s1, T), at(s2, T), o1, o2), m, **kw)

    def tt(out, a, b, op, m, **kw):
        vec(lambda T, e: e.tensor_tensor(out(T), a(T), b(T), op), m, **kw)

    def cp(out, src, m, **kw):
        vec(lambda T, e: e.tensor_copy(out(T), src(T)), m, **kw)

    def scan(out, d0, d1, first, o0, o1, m, **kw):
        vec(lambda T, e: e.tensor_tensor_scan(out(T), d0(T), d1(T), first, o0, o1), m, **kw)

    def act(out, src, func, m, bias=None, scale=None, acc_out=None, kind="v", **kw):
        def f(g, T, e):
            k = {}
            if bias is not None:
                k["bias"] = at(bias, T)
            if scale is not None:
                k["scale"] = at(scale, T)
            if acc_out is not None:
                k["accum_out"] = acc_out(T)
            return e.activation(out(T), src(T), func, **k)
        add("S", (kind, m), f, **kw)

    def pe(mms, **kw):
        def f(g, T, e):
            for o, l, r, s0, s1, _c in mms:
                x = e.matmul(o(T), l(T), r(T), s0, s1)
            return x
        add("P", ("p", [m[5] for m in mms]), f, **kw)

    def group(out, pairs, cols):
        return [(out, l, r, i == 0, i == len(pairs) - 1, cols) for i, (l, r) in enumerate(pairs)]
    return vec, ts, tt, cp, scan, act, pe, group


def build():
    ops = []
    CUR["lc"] = (-1, 0)

    def add(eng, c, fn, rd=(), wr=(), bank=(), name="", sem=None, inc=1, acc=None):
        op = {"e": eng, "c": c, "fn": fn, "rd": list(rd), "wr": list(wr), "bank": list(bank), "name": name or str(wr[0]),
              "sem": sem, "inc": inc, "lc": CUR["lc"], "acc": acc, "id": len(ops)}
        op["dur"], op["lat"] = cost(op, CFG)
        ops.append(op)
    vec, ts, tt, cp, scan, act, pe, group = tools(add)

    def load(q, dst, src, w, key, lat):
        add(q, ("dma", lat), lambda g, T, e: e.dma_start(T[dst][:, 0:w], T[src][:]), wr=[dst] if dst != "zb" else [("zb", 0, c) for c in range(NCH)],
            name="load " + src, sem="ld_" + key, inc=16, acc=("load", q))
    load("D", "rkb", "rk", C, "rk", 2.0)
    load("E", "zb", "z0", C, "z", 2.0)
    load("E", "wtb", "wt", 1, "wt", 2.0)
    load("D", "gearb", "gx", VX, "gear", 3.6)
    load("D", "rtb", "rt", 2 * C, "rt", 4.3)
    load("D", "siteb", "sy", VY, "site", 7.0)
    load("D", "thb", "th", 1, "th", 7.0)
    load("D", "wri", "wr", 2 * C, "wr", 7.7)

    def aff(dst, src, m, pat, cmp_, base, cm, a=0, other=0.0):
        add("G", ("G", m), lambda g, T, e: e.affine_select(T[dst][:, a:a + m], T[src][:, 0:m], pat, cmp_, other, base, cm),
            rd=[src], wr=[dst if a == 0 else (dst, a)], name="aff " + dst, acc="G")

    def iot(dst, m, pat, base, cm):
        def f(g, T, e):
            if SCRATCH[dst][2] == "int32":
                return e.iota(T[dst][:, 0:m], pat, base, cm)
            return e.iota(T[dst][:, 0:m], pat, base, cm, allow_small_or_imprecise_dtypes=True)
        add("G", ("G", m), f, wr=[dst], name="iota " + dst, acc="G")

    def fill(dst, ap, v, m, rd=(), wr=None):
        vec(lambda T, e: e.memset(ap(T), v), m, rd=rd, wr=wr or [dst])

    def cst(dst, src, m, mul, addv=None, a=0, rd=()):
        ts(M(dst, a, m), M(src, 0, m), mul, addv, OP.mult, None if addv is None else OP.add, m // 2, rd=[src] + list(rd), wr=[dst if a == 0 else (dst, a)])

    def sca(dst, src, m, mul, addv=None, a=0, rd=()):
        act(M(dst, a, m), M(src, 0, m), AF.Copy, m, bias=addv, scale=mul, rd=[src] + list(rd), wr=[dst if a == 0 else (dst, a)])

    fill("one", M("one", 0, 144), 1.0, 72)
    fill("m64", M("m64", 0, 1024), -64.0, 512)
    iot("kf", 1, [[0, 1]], 0, 1)
    aff("idn", "one", 128, [[-1, 128]], OP.is_equal, 0, 1)
    aff("tmpa", "one", 144, [[-16, 9], [0, 16]], OP.is_ge, 0, 1)
    aff("tmpb", "tmpa", 144, [[16, 9], [0, 16]], OP.is_ge, 15, -1)
    aff("b1", "tmpb", 144, [[0, 9], [1, 16]], OP.is_equal, -15, 0)
    iot("io1", nq, [[32, nq]], 0, 0)
    sca("blkm", "tmpb", 128, -1.0)
    iot("j1", 128, [[0, 16], [2, 8]], 1, 0)
    iot("s3", 128, [[0, 8], [2, 16]], -15, 0)
    aff("low", "blkm", 128, [[1, 128]], OP.is_ge, -1, -1)
    aff("upp", "blkm", 128, [[-1, 128]], OP.is_ge, -1, 1)
    aff("m1f", "low", 128, [[-1, 128]], OP.not_equal, 0, 1, other=-32.0)
    aff("m2f", "upp", 128, [[-1, 128]], OP.not_equal, 0, 1, other=64.0)
    for a in range(2):
        aff("bkh", "m64", 1024, [[-1, 8], [-16, 8], [0, 16]], OP.is_equal, -8 * a, 1, a=1024 * a)
    iot("own", 128, [[0, 16], [512, 8]], 384, 0)
    for t_ in range(8):
        aff("bo", "own", 128, [[-8, 16], [0, 8]], OP.is_equal, -t_, 1, a=128 * t_)
    aff("bs", "m64", 1024, [[-1, 8], [-8, 16], [0, 8]], OP.is_equal, 0, 1)
    ts(col("k15"), col("kf"), 15, None, OP.bitwise_and, None, 1, rd=["kf"], wr=["k15"])
    ts(col("k8"), col("kf"), 7, None, OP.bitwise_and, None, 1, rd=["kf"], wr=["k8"])
    cst("cz", "k15", 1, 1.0)
    cst("cj", "k8", 1, 2.0, 1.0)
    ts(M("io2", 0, nq), M("io1", 0, nq), col("cz"), col("cz"), OP.add, OP.add, nq, rd=["io1", "cz"], wr=["io2"])
    for c in range(NCH):
        cp(M("lst", c * n, n), M("rkb", c * n, n), n, rd=["rkb"], wr=[("lst", 0, c)], name="lst0")
    cst("wcol", "wtb", 1, 1.0)
    cst("bw", "b1", 144, col("wcol"), rd=["wcol"])
    w37 = 37.0 * 32 if UMOD else 37.0
    cst("wa", "wtb", 1, w37)
    cst("wac", "wa", 1, 1.0)
    ts(col("wb"), col("wtb"), w37, col("wac"), OP.mult, OP.subtract, 1, rd=["wtb", "wac"], wr=["wb"])
    cst("lwa", "tmpb", 128, col("wac"), rd=["wac"])
    cst("lwb", "tmpb", 128, col("wb"), rd=["wb"])
    if UMOD:
        cst("lw", "tmpb", 128, col("wcol"), rd=["wcol"])
        sca("iq", "idn", 128, -37.0 * 2 ** 17)
        sca("icq", "idn", 128, 37.0 * 2 ** 24)
    for nm, x in (("idm", -1.0), ("im16", -16.0), ("i16", 16.0), ("i32", 32.0), ("ih", 0.5), ("im2", -2.0)):
        sca(nm, "idn", 128, x)
    for a, (x, y) in enumerate(((-8.0, 0.5), (-7.5, -0.5))):
        sca("ta", "idn", 128, x, a=128 * a)
        sca("tb", "idn", 128, y, a=128 * a)
    for nm, x, y in (("ca", -512.0, None), ("cs", -32.0, None), ("ck2", 0.5, None), ("cb1", 1.5, 81.0)):
        cst(nm, "cz", 1, x, y)
    ts(col("cub"), col("cz"), 8.0, -(0.5 - 2.0 ** -12), OP.is_ge, OP.mult, 1, rd=["cz"], wr=["cub"])
    cst("ct", "thb", 1, -1.0, 2048.0)
    cst("tdg", "idn", 128, col("ct"), rd=["ct"])
    fill("rsc1", M("rsc"), 1.0, 64)
    fill("rsc", M("rsc", 15, 8, 16), 0.0, 8, wr=["rsc", "rsc1"])
    for c in range(NCH):
        fill("d0a", M("d0a", 6 * c * n, 3 * n), 0.0, 3 * n // 2, wr=[("d0a", c)])
    fill("d0b", M("d0b", 0, C, 3), 0.0, C // 2, wr=[("d0b", c) for c in range(NCH)])
    ts(M("d1", 2, C, 3), M("m64", 0, C), 0.0, None, OP.mult, None, C // 2, rd=["m64"], wr=[("d1", c) for c in range(NCH)], name="d1")
    cst("s1", "idn", 128, col("cb1"), rd=["cb1"])
    cst("lowh", "low", 128, 0.5)
    tt(M("m1h"), M("s1"), M("lowh"), OP.add, 256, rd=["s1", "lowh"], wr=["m1h"])
    cst("uph", "upp", 128, 0.5)
    fill("one32", M("one32"), 1.0, 128)
    ts(M("rst", 0, 512), M("m64", 0, 512), -8.0, None, OP.mult, None, 256, rd=["m64"], wr=["rst1"])
    ts(M("rst", 0, 64, 8), M("m64", 0, 64), -1.0, None, OP.mult, None, 64, rd=["m64"], wr=["rst", "rst1"])
    cst("j2", "j1", 128, -1.0, -1.0)
    tt(M("j3"), M("j1"), M("j2"), OP.mult, 256, rd=["j1", "j2"], wr=["j3"])
    tt(M("oth"), M("j3"), M("tmpb"), OP.mult, 256, rd=["j3", "tmpb"], wr=["oth"])
    for j in range(2):
        b = 4 + 2 + j
        ms = []
        for k in range(4):
            ms += group(PS(b, 128 * k, 128), [(M("idn"), M("bo", 512 * j + 128 * k)), (M("idn"), M("oth"))], 128)
        pe(ms, rd=["idn", "oth", "bo"] + [("bo", 128 * x) for x in range(1, 4 * j + 4)], wr=[("bap", j)], bank=[b], name="bap")
        cp(M("ba", 512 * j, 512), PS(b, 0, 512), 512, rd=[("bap", j)], wr=[("ba", j)], bank=[b], name="ba")
    act(M("s4"), M("s3"), AF.Abs, 128, rd=["s3"], wr=["s4"])
    ts(M("s5"), M("s4"), col("cj"), None, OP.is_equal, None, 64, rd=["s4", "cj"], wr=["s5"])
    ts(M("s6"), M("s3"), -2048.0, 1.0, OP.mult, OP.max, 64, rd=["s3"], wr=["s6"])
    ts(M("s4"), M("s6"), 2048.0, None, OP.min, None, 64, rd=["s6"], wr=["s4"])
    tt(M("s6"), M("s4"), M("s5"), OP.mult, 256, rd=["s4", "s5"], wr=["s6"])
    tt(M("wn"), M("s6"), M("tmpb"), OP.mult, 256, rd=["s6", "tmpb"], wr=["wn"])

    for e_ in range(LE):
        for c in range(NCH):
            CUR["lc"] = (e_, c)
            chunk(add, e_, c)
    return ops


def chunk(add, e_, c):
    vec, ts, tt, cp, scan, act, pe, group = tools(add)
    i0 = c * n
    pr = e_ % 2
    o = pr * C + i0
    of = 16 * o
    R0, R1, X0, X1 = 4 * (c % 2), 4 * (c % 2) + 1, 4 * (c % 2) + 2, 4 * (c % 2) + 3
    lz = e_ * C + i0
    ot = (pr * NCH + c) * nq
    last = e_ == LE - 1
    t = lambda nm, *x: (nm, pr, c) + x
    L, Z = ("lst", e_, c), ("zb", e_, c)
    IND = lambda win, a, w, off, b, k: (lambda T: T[win][:, a:a + w].indirect(T[off][:, b:b + k]))
    blocks = [(s, sum(XB[:s]), w) for s, w in enumerate(XB)]
    xblocks = [(s, sum(XG[:s]), w) for s, w in enumerate(XG)]
    XX = [t("xx", s) for s, a, w in xblocks]
    G0, G1 = ("grp", R0), ("grp", R1)

    pe([(PS(R0, 0, nq), M("bw", 15 - m), M("zb", lz + m, nq, 16), m == 0, m == 15, nq) for m in range(16)],
       rd=["bw", Z], wr=[t("ul")], bank=[R0], acc=G0, name="UL")
    cp(M("ci", ot, nq), PS(R0, 0, nq), nq, rd=[t("ul")], wr=[t("ci")], bank=[R0], name="ci")
    ts(M("v5", ot, nq), M("ci", ot, nq), 31, None, OP.bitwise_and, None, nq, rd=[t("ci")], wr=[t("v5")], name="v5")
    tt(M("vv", ot, nq), M("v5", ot, nq), M("v5", ot, nq), OP.mult, nq, rd=[t("v5")], wr=[t("vv")], name="vv")
    ts(M("bi", ot, nq), M("vv", ot, nq), 5, 1, OP.arith_shift_right, OP.bitwise_and, nq, rd=[t("vv")], wr=[t("bi")], name="bi")
    tt(M("cc", ot, nq), M("bi", ot, nq), M("io2", 0, nq), OP.add, nq, rd=[t("bi"), "io2"], wr=[t("cc")], name="cc")
    cp(M("cl", o, nq), M("cc", ot, nq), nq, rd=[t("cc")], wr=[t("cl")], name="cl")
    u37 = [(M("lwa"), M("zb", lz, n)), (M("lwb"), M("zb", lz, n))]
    if UMOD:
        pe(group(PS(R1, 128, n), [(M("lw"), M("zb", lz, n))], n), rd=["lw", Z], wr=[t("u0")], bank=[R1], acc=G1, name="U0")
        act(M("uh", o, n), PS(R1, 128, n), AF.Copy, n, bias=128.0, scale=1.0 / 4096, rd=[t("u0")], wr=[t("uh")], bank=[R1], name="uh")
        u37 = [(M("one"), M("icq")), (M("iq"), M("uh", o, n))] + u37
    pe(group(PS(R0, 128, n), u37, n), rd=["lwa", "lwb", Z] + (["one", "icq", "iq", t("uh")] if UMOD else []), wr=[t("u37")], bank=[R0], acc=G0, name="U37")

    ts(M("k32", o, n), M("lst", lz, n), 32.0, None, OP.add, None, n, rd=[L], wr=[t("k32")], name="k32")
    for s, a, w in xblocks:
        act(M("xx", of + a * 16, w * 16), IND("gearb", 0, VX, "lst", lz + a, w), AF.Copy, w * 16, kind="g", rd=["gearb", L], wr=[t("xx", s)], name="x")
    tt(M("pp", o, n), IND("rtb", 2 * i0, 2 * n, "cl", o, nq), M("k32", o, n), OP.mult, n, kind="g", rd=["rtb", t("cl"), t("k32")], wr=[t("pp")], name="P")
    if UMOD:
        tt(M("tt", o, n), M("pp", o, n), PS(R0, 128, n), OP.add, n, rd=[t("pp"), t("u37")], wr=[t("tt")], bank=[R0], name="T")
        ts(M("t2", o, n), M("tt", o, n), 5, 4095, OP.arith_shift_right, OP.bitwise_and, n, rd=[t("tt")], wr=[t("t2")], name="T2")
    else:
        ts(M("qq", o, n), M("pp", o, n), 5, None, OP.arith_shift_right, None, n, rd=[t("pp")], wr=[t("qq")], name="Q")
        tt(M("tt", o, n), M("qq", o, n), PS(R0, 128, n), OP.add, n, rd=[t("qq"), t("u37")], wr=[t("tt")], bank=[R0], name="T")
        ts(M("t2", o, n), M("tt", o, n), 4095, None, OP.bitwise_and, None, n, rd=[t("tt")], wr=[t("t2")], name="T2")
    cp(M("sl", o, n), M("t2", o, n), n, rd=[t("t2")], wr=[t("sl")], name="SL")

    for j in range(NB):
        b = (X0, X1)[j % 2]
        ms = []
        for kk in range(KB):
            k = j * KB + kk
            ms += group(PS(b, kk * n, n), [(M("idn"), M("xx", of + k, n, 16)), (M("idm"), M("zb", lz, n))], n)
        pe(ms, rd=["idn", "idm", Z] + XX, wr=[t("xz", j)], bank=[b], acc=("grp", b), name="xz")
        for h in range(KB // 2):
            k = j * KB + 2 * h
            act(M("sg", of + k * n, 2 * n), PS(b, 2 * h * n, 2 * n), AF.Sign, 2 * n, bias=0.5 - 16 * ((15 - k) // 2), rd=[t("xz", j)], wr=[t("sg", k // 2)],
                bank=[b], name="sg")
        ms = [(PS(R1, 0, 128), M("one"), M("im16"), True, False, 128)] if j == 0 else []
        ms += [(PS(R1, k, 8, 16), M("sg", of + k * n, n), M("tmpb", 0, 8, 16), False, False, 8) for k in range(j * KB, j * KB + KB)]
        pe(ms, rd=["one", "im16", "tmpb"] + [t("sg", v) for v in range(j * KB // 2, j * KB // 2 + KB // 2)], wr=[t("cn", j)], bank=[R1], acc=G1, name="cnt")

    ms = [(PS(R0, 256, 128), M("one"), M("tdg"), True, False, 128)]
    rv = [b for b in blocks if (c, b[0]) in RELU_V]
    for s, a, w in blocks:
        a, w, a0, w0 = of + a * 16, w * 16, a, w
        tt(M("dd", a, w), IND("siteb", 0, VY, "sl", o + a0, w0), M("xx", a, w), OP.subtract, w, kind="g", rd=["siteb", t("sl")] + [t("xx", x) for x, xa, xw in xblocks if xa < a0 + w0 and xa + xw > a0], wr=[t("dd", s)], name="y")
        if (c, s) in RELU_V:
            ts(M("da", a, w), M("dd", a, w), 0.0, 2.0, OP.max, OP.mult, w // 2, rd=[t("dd", s)], wr=[t("da", s)], name="relu")
        else:
            act(M("da", a, w), M("dd", a, w), AF.Abs, w, rd=[t("dd", s)], wr=[t("da", s)], name="abs")
    if rv:
        p0, pw = rv[0][1], sum(b[2] for b in rv)
        ms += [(lambda T, k=k: T["ps%d" % R0][p0:p0 + pw, 256 + k:256 + 128:16], M("dd", of + 16 * p0 + k, pw, 16), M("blkm", 0, 8, 16), False, False, 8) for k in range(16)]
    pe(ms, rd=["one", "tdg", "blkm"] + [t("dd", b[0]) for b in rv], wr=[t("D0")], bank=[R0], acc=G0, name="D0")
    pe([(PS(R0, 256 + k, 8, 16), M("da", of + k, n, 16), M("tmpb", 0, 8, 16), False, k == 15, 8) for k in range(16)],
       rd=["tmpb"] + [t("da", s) for s, a, w in blocks], wr=[t("D")], bank=[R0], acc=G0, name="D")
    act(M("pm", o, n), PS(R0, 256, n), AF.Sign, n, bias=2047.5 if e_ == 0 else M("tac", e_, 1), scale=-1.0, rd=[t("D")] + ([("tac", e_)] if e_ else []), wr=[t("pm")],
        bank=[R0], name="p")
    pe([(PS(R1, 0, 128), M("i16"), M("pm", o, n), False, True, n)], rd=["i16", t("pm")], wr=[t("cn")], bank=[R1], acc=G1, name="cnp")
    pe([(PS(R0, 0, 2 * n), M("pm", o, n), M("ta", 0, 256), True, False, 2 * n)], rd=["ta", ("ta", 128), t("pm")], wr=[t("N0")], bank=[R0], acc=G0, name="N0")
    scan(REV("sv", o, n), REV("rsc", 0, n), REV("ps%d" % R1, 0, n), 0.0, OP.mult, OP.max, n, rd=["rsc", t("cn")], wr=[t("sv")], bank=[R1], name="stop")
    pe([(PS(R0, 0, 2 * n), M("sv", o, n), M("tb", 0, 256), False, True, 2 * n)], rd=["tb", ("tb", 128), t("sv")], wr=[t("N")], bank=[R0], acc=G0, name="N")
    DA, DB, D1 = ("d0a", c), ("d0b", c), ("d1", c)
    HS = lambda a=0, w=n: M("d0a", 6 * i0 + 3 * n + 1 + 3 * a, w, 3)
    NF = M("d0a", 6 * i0 + 1, n, 3)
    act(M("d0a", 6 * i0 + 1, 2 * n, 3), PS(R0, 0, 2 * n), AF.Sign, 2 * n, bias=8.0, rd=[t("N")], wr=[DA], bank=[R0], name="nfh")
    act(M("d0b", 3 * i0 + 1, n, 3), PS(R0, 0, n), AF.Relu, n, bias=-7.0, scale=-1.0, acc_out=None if last else M("fs", e_ * NCH + c, 1), rd=[t("N")],
        wr=[DB, ("fs", e_, c)], bank=[R0], name="f")
    pe(group(PS(R1, 128, n), [(M("m1f"), NF), (M("m1h"), HS())], n) + group(PS(R1, 128 + n, n), [(M("m2f"), NF), (M("i32"), HS())], n),
       rd=["m1f", "m1h", "m2f", "i32", DA], wr=[t("E")], bank=[R1], acc=G1, name="E")
    act(M("rr", 2 * o, 2 * n), PS(R1, 128, 2 * n), AF.Relu, 2 * n, bias=-81.0, rd=[t("E")], wr=[t("rr")], bank=[R1], name="R")
    pos = [(M("uph"), HS()), (M("idn"), M("rr", 2 * o, n)), (M("idn"), M("rr", 2 * o + n, n))]
    PV = R0 if POS2 else R1
    if POS2:
        pe(group(PS(R0, 384, n), pos, n), rd=["uph", "idn", DA, t("rr")], wr=[t("pv")], bank=[R0], acc=G0, name="POSv")
    pe(group(PS(R1, 384, n), pos, n), rd=["uph", "idn", DA, t("rr")], wr=[t("po")], bank=[R1], acc=G1, name="POS")
    ts(M("d0b", 3 * i0 + 2, n, 3), PS(PV, 384, n), col("ck2"), 2.0 ** -11, OP.is_ge, OP.max, n, rd=[t("pv" if POS2 else "po"), "ck2"], wr=[DB], bank=[PV], name="mult")
    act(M("aa", o, n), PS(R1, 384, n), AF.Abs, n, bias=col("ca"), scale=1024.0, rd=[t("po"), "ca"], wr=[t("aa")], bank=[R1], name="a")
    act(M("ss", o, n), PS(R1, 384, n), AF.Square, n, bias=col("cs"), scale=64.0, rd=[t("po"), "cs"], wr=[t("ss")], bank=[R1], name="s")
    if e_ == 0:
        cp(M("wrb", 2 * i0, 2 * n), M("wri", 2 * i0, 2 * n), 2 * n, rd=["wri"], wr=[("wrb", c)], name="wrb")
    cp(M("d1", 3 * i0 + 1, n, 3), M("lst", lz, n), n // 2, rd=[L], wr=[D1], name="k16")
    tt(M("d1", 3 * i0, n, 3), IND("wrb", 2 * i0, 2 * n, "cl", o, nq), M("d1", 3 * i0 + 1, n, 3), OP.subtract, n, kind="g", rd=[("wrb", c), t("cl")], wr=[D1], name="dk")
    scan(M("ob", 3 * o, 3 * n), M("d0b", 3 * i0, 3 * n), M("d1", 3 * i0, 3 * n), 0.0, OP.mult, OP.subtract, 3 * n // 2, rd=[DB, D1], wr=[t("ob")], name="v")

    def held(bb, q):
        b = ((X0, X1)[q] + 4 * bb * XMX) % 8
        pe([(PS(b, kk, 64, 8), M("ih"), M("xx", of + 1024 * bb + 8 * q + kk, 64, 16), kk == 0, False, 64) for kk in range(8)],
           rd=["ih"] + XX, wr=[t("xp", bb, q)], bank=[b], acc=("grp", b), name="xp")
        pe([(PS(b, kk, 64, 8), M("bkh", 128 * (8 * q + kk)), HS(64 * bb, 64), False, kk == 7, 64) for kk in range(8)],
           rd=[("bkh", 1024) if q else "bkh", DA], wr=[t("xm", bb, q)], bank=[b], acc=("grp", b), name="xm")
        a = of + 512 * bb
        if not ESPLIT:
            scan(M("xs", a + 8 * n * q, 512), M("rst", 0, 512), PS(b, 0, 512), 64.0, OP.min, OP.max, 512, rd=["rst", t("xm", bb, q)], wr=[t("xs", bb, q)],
                 bank=[b], name="scan")
        elif q == 0:
            act(M("xs", a + 8 * n, 512), PS(b, 0, 512), AF.Copy, 512, rd=[t("xm", bb, q)], wr=[t("xs", bb, 1)], bank=[b], name="ev")
        else:
            tt(M("xs", a + 8 * n, 512), M("xs", a + 8 * n, 512), PS(b, 0, 512), OP.max, 512, rd=[t("xm", bb, q)], wr=[t("xs", bb, 1)], bank=[b], name="pair")
            scan(M("xs", a, 512), M("rst", 0, 512), M("xs", a + 8 * n, 512), 64.0, OP.min, OP.max, 256, rd=["rst", t("xs", bb, 1)], wr=[t("xs", bb, 0)], name="scan")

    def pick(j):
        b = ((X0, X1)[j % 2] + 4 * CDX) % 8
        k0, PW = sum(x[1] for x in PICK[:j]), PICK[j][1]
        ms = []
        for kk in range(PW):
            k = k0 + kk
            ms += group(PS(b, kk * n, n), [(M("ba", 128 * k), M("aa", o, n)), (M("bs", 128 * k), M("ss", o, n)), (M("bs", 128 * k), M("ob", 3 * o + 2, n, 3))], n)
        pe(ms, rd=[("ba", 0), ("ba", 1), "bs", t("aa"), t("ss"), t("ob")], wr=[t("cd", j)], bank=[b], acc=("grp", b), name="cd")
        a, w = 8 * o + k0 * n, PW * n
        if PICK[j][0] == "S":
            act(M("kl", a, w), PS(b, 0, w), AF.Relu, w, scale=1.0 / 64, rd=[t("cd", j)], wr=[t("kl", j)], bank=[b], name="pick")
        else:
            ts(M("kl", a, w), PS(b, 0, w), 0.0, 1.0 / 64, OP.max, OP.mult, w, rd=[t("cd", j)], wr=[t("kl", j)], bank=[b], name="pick")
        pe([(PS(R1, 0, n), M("wn"), M("kl", 8 * o + k * n, n), k == 0, k == 7, n) for k in range(k0, k0 + PW)], rd=["wn", t("kl", j)],
           wr=[t("nm") if j == len(PICK) - 1 else t("nm", j)], bank=[R1], acc=G1, name="NM")

    for j in range(HELD1):
        held(j // 2, j % 2)
    if HELD1 < 4:
        for j in range(len(PICK)):
            pick(j)
    for j in range(HELD1, 4):
        held(j // 2, j % 2)
    XS = [t("xs", bb, q) for bb in range(n // 64) for q in range(2)]
    if not ESPLIT:
        tt(M("mm", o, n), M("xs", of + 7, n, 8), M("xs", of + 8 * n + 7, n, 8), OP.max, 2 * n, rd=XS, wr=[t("mm")], name="mm")
    pe(group(PS(R0, 256, n), [(M("idn"), M("zb", lz, n)), (M("im2"), M("xs", of + 7, n, 8) if ESPLIT else M("mm", o, n))], n), rd=["idn", "im2", Z, t("mm")] + XS, wr=[t("zn")], bank=[R0], acc=G0, name="ZN")
    act(M("zsend", lz, n), PS(R0, 256, n), AF.Abs, n, bias=128.0, rd=[t("zn")], wr=[("zsend", e_, c)], bank=[R0], name="z'")
    if not last and c == NCH - 1:
        pe(group(PS(FB, 0, NCH), [(M("one32"), M("fs", e_ * NCH, NCH))], 256), rd=["one32"] + [("fs", e_, x) for x in range(NCH)],
           wr=[("f2", e_)], bank=[FB], acc=G0, name="F2")
        ts(M("fi", e_, 1), PS(FB, 0, 1), PS(FB, 1, 1), None, OP.add, None, 1, rd=[("f2", e_)], wr=[("fi", e_)], bank=[FB], name="fi")
        ts(M("fm", e_, 1), M("fi", e_, 1), 31, None, OP.bitwise_and, None, 1, rd=[("fi", e_)], wr=[("fm", e_)], name="fm")
        ts(M("tac", e_ + 1, 1), M("fm", e_, 1), 16.0, 2047.5, OP.mult, OP.add, 1, rd=[("fm", e_)], wr=[("tac", e_ + 1)], name="ta")
    if HELD1 == 4:
        for j in range(len(PICK)):
            pick(j)
    ts(M("ui", o, n), PS(R1, 0, n), col("cub"), None, OP.add, None, n, rd=[t("nm"), "cub"], wr=[t("ui")], bank=[R1], name="ui")
    ts(M("uj", o, n), M("ui", o, n), 2047, None, OP.bitwise_and, None, n, rd=[t("ui")], wr=[t("uj")], name="uj")
    scan(M("oa", 3 * o, 3 * n), M("d0a", 6 * i0, 3 * n), M("d1", 3 * i0, 3 * n), 0.0, OP.mult, OP.add, 3 * n // 2, rd=[DA, D1], wr=[t("oa")], name="w'")
    cp(IND("wrb", 2 * i0, 2 * n, "cl", o, nq), M("oa", 3 * o + 1, n, 3), n, kind="s", rd=[t("cl"), t("oa")], wr=[("wrb", c)], name="scat")
    if not last:
        cp(M("lsend", lz, n), M("uj", o, n), n, rd=[t("uj")], wr=[("lsend", e_, c)], name="K'")
        for kind, src, dst in (("z", "zsend", "zb"), ("k", "lsend", "lst")):
            add("G", ("net", 0), lambda g, T, e, src=src, dst=dst: [(T[dst][:, lz + C:lz + C + n], T[src][:, lz:lz + n])],
                rd=[(src, e_, c)], wr=[(dst, e_ + 1, c)], name="send" + kind, sem="a%s%d_%d" % (kind, e_ + 1, c), inc="net")
    else:
        cp(M("yks", i0, n), M("uj", o, n), n, rd=[t("uj")], wr=[("yks", c)], name="yk")
        for q, (dst, src, tok, a, w, sa) in enumerate((("yz", "zsend", ("zsend", e_, c), i0, n, lz), ("yw", "wrb", ("wrb", c), 2 * i0, 2 * n, 2 * i0),
                                                       ("yk", "yks", ("yks", c), i0, n, i0))):
            add("D", ("dma", 2.0), lambda g, T, e, dst=dst, src=src, a=a, w=w, sa=sa: e.dma_start(T[dst][:, a:a + w], T[src][:, sa:sa + w]), rd=[tok], wr=[(dst, c)],
                name="store " + dst, sem="st%d" % (3 * c + q), inc=16)


def depend(ops):
    wrote, readers, banks, last = {}, {}, {}, {}
    for i, op in enumerate(ops):
        d = set()
        for k in op["rd"]:
            if k in wrote:
                d.add(wrote[k])
        for k in op["wr"]:
            if k in wrote:
                d.add(wrote[k])
            d |= readers.get(k, set())
        for b in op["bank"]:
            h = banks.setdefault(b, [])
            for j in h[-40:]:
                if ops[j]["e"] != op["e"]:
                    d.add(j)
            h.append(i)
        for k in op["rd"]:
            readers.setdefault(k, set()).add(i)
        for k in op["wr"]:
            wrote[k] = i
            readers[k] = set()
        d.discard(i)
        op["dep"] = d
        op["ord"] = set()
        if op["acc"] is not None:
            if op["acc"] in last:
                op["ord"].add(last[op["acc"]])
            last[op["acc"]] = i


def order(ops):
    place, early, seen, key = {}, {}, {}, []
    words = ROUND.split()
    for p, w in enumerate(words):
        place[w.strip("<>")] = p + len(words) * (w.count(">") - w.count("<"))
    wait = []
    for w in START.split():
        if w[0] == "|":
            nm, i = w[1:].split(":")
            for j, x in enumerate(wait):
                early[x] = place[nm] + len(words) * int(i) - 0.9 + 0.01 * j
            wait = []
        else:
            wait.append(w)
    for op in ops:
        e, c = op["lc"]
        k = seen.get((e, c, op["name"]), 0)
        seen[(e, c, op["name"])] = k + 1
        u = op["name"] + (str(k) if k else "")
        u = u.replace("store ", "st_").replace("load ", "ld_").replace("aff ", "").replace("iota ", "").replace("('", "").replace("', ", "_").replace(")", "")
        key.append(early[u] if e < 0 else place[u] + len(words) * (NCH * e + c))
    succ = [[] for _ in ops]
    left = []
    for i, op in enumerate(ops):
        left.append(len(op["dep"] | op["ord"]))
        for j in op["dep"] | op["ord"]:
            succ[j].append(i)
    ready = [i for i in range(len(ops)) if left[i] == 0]
    seq = []
    while ready:
        i = min(ready, key=lambda x: (key[x], x))
        ready.remove(i)
        seq.append(i)
        for j in succ[i]:
            left[j] -= 1
            if left[j] == 0:
                ready.append(j)
    return seq, 0.0


def order_greedy(ops):
    N_ = len(ops)
    succ = [[] for _ in range(N_)]
    for i, op in enumerate(ops):
        for j in op["dep"] | op["ord"]:
            succ[j].append(i)
    wake = CFG["wake"]
    prio = [0.0] * N_
    for i in range(N_ - 1, -1, -1):
        e, c = ops[i]["lc"]
        if e >= 0:
            prio[i] = ops[i]["dur"] + ops[i]["lat"] + max([prio[j] + wake for j in succ[i] if ops[j]["lc"][1] == c] or [0.0])
    top = {}
    for i in range(N_):
        if ops[i]["name"] == "k32":
            top[ops[i]["lc"]] = prio[i]
    for i in range(N_ - 1, -1, -1):
        e, c = ops[i]["lc"]
        if e >= 0:
            prio[i] += (LE - e - c / NCH) * CFG["T"] - top[(e, c)] + BIAS.get((ops[i]["name"], c), BIAS.get(ops[i]["name"], 0.0)) + BIAS.get((e, c), 0.0)
        else:
            prio[i] = ops[i]["dur"] + ops[i]["lat"] + max([prio[j] + wake for j in succ[i]] or [0.0])
    free, done, left = {}, [0.0] * N_, [len(op["dep"] | op["ord"]) for op in ops]
    qu = [{"E": "S"}.get(op["e"], op["e"]) for op in ops]
    ready = {}
    rt = [0.0] * N_
    for i in range(N_):
        if left[i] == 0:
            ready.setdefault(qu[i], []).append(i)
    seq = []
    while len(seq) < N_:
        best = None
        for q, lst in ready.items():
            if not lst:
                continue
            m = max(free.get(q, 0.0), min(rt[i] for i in lst))
            if best is None or m < best[0]:
                best = (m, q)
        m, q = best
        i = max((x for x in ready[q] if rt[x] <= m + 1e-9), key=lambda x: prio[x])
        soon = [x for x in ready[q] if prio[x] > prio[i] + CFG["gap"] and rt[x] <= m + CFG["look"] * ops[i]["dur"]]
        if soon:
            i = min(soon, key=lambda x: rt[x])
            m = max(m, rt[i])
        ready[q].remove(i)
        op = ops[i]
        end = m + op["dur"]
        free[q] = end
        op["start"] = m
        done[i] = end + op["lat"]
        seq.append(i)
        for j in succ[i]:
            left[j] -= 1
            rt[j] = max(rt[j], done[i] + wake if i in ops[j]["dep"] else end)
            if left[j] == 0:
                ready.setdefault(qu[j], []).append(j)
    return seq, max(done)


def plan():
    if "p" not in CACHE:
        ops = build()
        depend(ops)
        seq, span = order(ops)
        cnt = {}
        know = {}
        clock = {}
        steps = []
        for i in seq:
            op = ops[i]
            q = {"E": "S"}.get(op["e"], op["e"])
            kn = know.setdefault(q, {})
            waits = {}
            for j in sorted(op["dep"], key=lambda x: -ops[x]["pos"]):
                s, v = ops[j]["at"]
                if kn.get(s, 0) < v:
                    waits[s] = max(waits.get(s, 0), v)
                    for s2, v2 in clock[j].items():
                        kn[s2] = max(kn.get(s2, 0), v2)
            op["pos"] = len(steps)
            if op["sem"] is None:
                s = {"V": "sV", "S": "sS", "P": "sP", "G": "sG"}[op["e"]]
                cnt[s] = cnt.get(s, 0) + 1
                op["at"] = (s, cnt[s])
            else:
                op["at"] = (op["sem"], op["inc"] if op["inc"] != "net" else 1)
            clock[i] = dict(kn) if op["inc"] != "net" else {}
            clock[i][op["at"][0]] = op["at"][1]
            steps.append((op, sorted(waits.items())))
        CACHE["p"] = (steps, cnt, span)
    return CACHE["p"]


def rank_program(g, core, T, topo):
    rank = T.rank_of(core)
    if rank is None:
        return
    nxt = T.cores[(rank + 1) % len(T.cores)]
    prv = T.cores[(rank - 1) % len(T.cores)]
    rid, pid, _se = topo.addr(nxt)
    eng = topo.engines(core, nxt)[:8]
    neng_in = len(topo.engines(prv, core)[:8])
    emask = 0
    for x in eng:
        emask |= 1 << x
    queues = {"V": g.vector, "S": g.scalar, "P": g.tensor, "G": g, "D": g.sync, "E": g.scalar}
    steps, cnt, span = plan()
    sent = 0
    for op, waits in steps:
        q = queues[op["e"]]
        for s, v in waits:
            q.wait_ge(T.sem[s], neng_in if s[0] == "a" else v)
        if op["inc"] == "net":
            for out, in_ in op["fn"](g, T, q):
                g.remote_dma(out, in_, T.sem[op["sem"]], T.sem.sent, pid, rid, emask)
                sent += len(eng)
        else:
            r = op["fn"](g, T, q)
            if op["sem"] is None:
                r.then_inc(T.sem[op["at"][0]], 1)
            else:
                r.then_inc(T.sem[op["sem"]], 16)
    for s, v in sorted(cnt.items()):
        g.wait_ge(T.sem[s], v)
    g.wait_ge(T.sem.sent, sent)
    for k in LOADS:
        g.wait_ge(T.sem["ld_" + k], 16)
    for k in range(3 * NCH):
        g.wait_ge(T.sem["st%d" % k], 16)
